import numpy as np
import ml_dtypes


def mxq(x, axis, fmt="e4m3"):
    dtype, down = {"e4m3": (ml_dtypes.float8_e4m3fn, 7), "e5m2": (ml_dtypes.float8_e5m2, 14)}[fmt]
    v = np.moveaxis(np.asarray(x, np.float32).astype(ml_dtypes.bfloat16).astype(np.float64), axis, -1)
    blocks = v.reshape(v.shape[:-1] + (-1, 32))
    amax = np.abs(blocks).max(-1, keepdims=True)
    byte = np.maximum(np.where(amax > 0, np.frexp(amax)[1] - 1 + 127, 0) - down, 1)
    scale = np.exp2(byte - 127.0)
    codes = (blocks / scale).astype(np.float32).astype(dtype).astype(np.float64)
    return np.moveaxis((codes * scale).reshape(v.shape), -1, axis)


WIDE = False


def mx_kscale(k):
    if not WIDE:
        return np.ones(k)
    levels = np.array([24, -24, 12, -12, 0])
    if k % 512:
        return np.exp2(np.random.permutation(np.resize(levels, k // 32))).repeat(32)
    a = np.empty((k // 512, 16))
    for p in range(k // 512):
        a[p, :8] = np.random.permutation(np.resize(levels, 8))
        for g in range(8):
            far = levels[np.abs(levels - a[p, g]) >= 10]
            a[p, g + 8] = far[np.random.randint(len(far))]
    return np.exp2(a.ravel()).repeat(32)


def f64(x):
    return np.asarray(x).astype(np.float64)


def striped8(idx):
    return np.concatenate([v.reshape(-1, 16).T for v in idx]).astype(np.uint16)


def unstriped8(offs):
    return np.stack([offs[16 * g:16 * g + 16].T.reshape(-1) for g in range(8)]).astype(np.int64)


E2M1 = np.array([0.0, 0.5, 1.0, 1.5, 2.0, 3.0, 4.0, 6.0, -0.0, -0.5, -1.0, -1.5, -2.0, -3.0, -4.0, -6.0])


def pack_weight(w, fmt):
    k, n = w.shape
    w = f64(np.asarray(w, np.float32).astype(ml_dtypes.bfloat16)).reshape(k // 32, 32, n)
    amax = np.abs(w).max(1)
    if fmt == "e4m3":
        byte = np.frexp(amax)[1] - 1 + 127 - 7
    else:
        mant, ex = np.frexp(amax / 6.0)
        byte = np.where(mant > 0.5, ex, ex - 1) + 127
    byte = np.clip(np.where(amax > 0, byte, 1), 1, 254)
    scaled = (w * np.exp2(127.0 - byte)[:, None, :]).reshape(k, n).astype(np.float32)
    by_word = np.ascontiguousarray(scaled.reshape(k // 512, 128, 4, n).transpose(0, 1, 3, 2))
    if fmt == "e4m3":
        words = by_word.astype(ml_dtypes.float8_e4m3fn).view(np.uint8)
    else:
        c = by_word.astype(ml_dtypes.float4_e2m1fn).view(np.uint8) & 0xF
        words = (c[..., 0::2] | (c[..., 1::2] << 4)).reshape(k // 512, 128, 2 * n)
    return np.ascontiguousarray(words), np.ascontiguousarray(byte.astype(np.uint8).reshape(k // 512, 16, n))


def unpack_weight(words, scales, fmt):
    g, _, n = scales.shape
    words = np.ascontiguousarray(words).reshape(g, 128, n, -1)
    if fmt == "e4m3":
        vals = words.view(ml_dtypes.float8_e4m3fn).astype(np.float64)
    else:
        nib = np.empty((g, 128, n, 4), np.uint8)
        nib[..., 0::2] = words & 0xF
        nib[..., 1::2] = words >> 4
        vals = E2M1[nib]
    vals = vals * np.repeat(np.exp2(scales.astype(np.float64) - 127.0), 8, axis=1)[..., None]
    return vals.transpose(0, 1, 3, 2).reshape(g * 512, n)


def planes(y):
    n, m = y.shape
    v = y.astype(np.float32).astype(ml_dtypes.bfloat16).astype(np.float64).reshape(n // 32, 32, m)
    top = np.abs(v).max(1)
    byte = np.clip(np.where(top > 0, np.frexp(top)[1] - 1 + 127 - 7, 1), 1, 254)
    codes = (v * np.exp2(127.0 - byte)[:, None, :]).reshape(n, m).astype(np.float32).astype(ml_dtypes.float8_e4m3fn).view(np.uint8)
    words = codes.reshape(n // 512, 128, 4, m).transpose(0, 1, 3, 2)
    return np.ascontiguousarray(words), np.ascontiguousarray(byte.astype(np.uint8).reshape(n // 512, 16, m))


def sigm(f):
    return 1.0 / (1.0 + np.exp(-np.maximum(f, -700.0)))


K, N, T, J = 512, 512, 2048, 1024


def setup_inputs():
    n = np.random.standard_normal
    s = mx_kscale(K)[:, None]
    p_wk = pack_weight(n((K, N)) / np.sqrt(K) / s, "e2m1")
    return {
        "xT": (n((K, T)) * s).astype(np.float32),
        "wgt": np.repeat(np.random.uniform(0.5, 2.0, (8, J)), 16, axis=0).astype(np.float32),
        "wk_words": p_wk[0],
        "wk_scales": p_wk[1],
        "wv": (n((K, N)) / np.sqrt(K) / s).astype(np.float32),
        "bg": (0.3 * n(N) - 1.0).astype(np.float32),
        "res": (n((N, J))).astype(np.float32),
        "offs": striped8(np.stack([np.random.permutation(T)[:J] for _ in range(8)])),
    }


def reference(xT, wgt, wk_words, wk_scales, wv, bg, res, offs):
    idx = unstriped8(offs)
    rows = np.arange(K)
    xg = f64(wgt)[rows // 4 % 128] * f64(xT)[rows[:, None], idx[rows % 512 // 64]]
    xT_ = mxq(xg, 0, "e4m3")
    wk_ = unpack_weight(wk_words, wk_scales, "e2m1")
    wv_ = mxq(f64(wv), 0, "e4m3")
    ke = wk_.T @ xT_
    ve = wv_.T @ xT_
    gate = sigm(ke + f64(bg)[:, None])
    out_0 = f64(res) + gate * (np.maximum(ve, 0.0) - f64(res))
    return (out_0,) + planes(out_0)

@@ -1,0 +1,210 @@
+from contextlib import ExitStack
+
+import concourse.mybir as mybir
+
+K, N, T, J = 512, 512, 2048, 1024
+FLOPS = 2 * 2 * K * N * J
+
+F32 = mybir.dt.float32
+BF16 = mybir.dt.bfloat16
+I32 = mybir.dt.int32
+U32 = mybir.dt.uint32
+U16 = mybir.dt.uint16
+U8 = mybir.dt.uint8
+FP8X4 = mybir.dt.float8_e4m3fn_x4
+FP4X4 = mybir.dt.float4_e2m1fn_x4
+ALU = mybir.AluOpType
+ACT = mybir.ActivationFunctionType
+
+P = 128
+PACK = 4
+C = 256
+CHUNKS = J // C
+
+
+def tile_list_hwayreluP_kernel(tc, xT, wgt, wk_words, wk_scales, wv, bg, res, offs, out_0, out_1, out_2):
+    nc = tc.nc
+    with ExitStack() as ctx:
+        keep = ctx.enter_context(tc.tile_pool(name="keep", bufs=1))
+        psum = ctx.enter_context(tc.psum_pool(name="psum", bufs=2))
+
+        offsets = keep.tile([P, J // 16], U16, name="offsets")
+        nc.sync.dma_start(offsets[:], offs)
+
+        wk_scale_raw = keep.tile([P, N], U8, name="wk_scale_raw", align_bytes=64)
+        nc.vector.memset(wk_scale_raw[:].bitcast(U32), 0)
+
+        wk_raw = keep.tile([P, 2 * N], U8, name="wk_raw", align_bytes=64)
+        nc.sync.dma_start(wk_raw[:].bitcast(I32), wk_words[0].bitcast(I32))
+        for q in range(4):
+            nc.scalar.dma_start(wk_scale_raw[32 * q : 32 * q + 4, :].bitcast(I32), wk_scales[0, 4 * q : 4 * q + 4, :].bitcast(I32))
+        warm = keep.tile([P, 1], F32, name="warm")
+        warm2 = keep.tile([P, 1], F32, name="warm2")
+        nc.vector.memset(warm[:], 0.0)
+        nc.scalar.activation(warm2[:], warm[:], ACT.Sigmoid)
+
+        weights = keep.tile([P, J], F32, name="weights")
+        x_rows = xT.rearrange("(p i) t -> p i t", i=PACK)
+        planes = [keep.tile([P, T], F32, name="plane%d" % i) for i in range(PACK)]
+        nc.sync.dma_start(weights[:, : J // 2], wgt[:, : J // 2])
+        nc.sync.dma_start(planes[0][:], x_rows[:, 0, :])
+        nc.sync.dma_start(weights[:, J // 2 :], wgt[:, J // 2 :])
+        nc.sync.dma_start(planes[1][:], x_rows[:, 1, :])
+        nc.sync.dma_start(planes[2][:], x_rows[:, 2, :])
+        nc.sync.dma_start(planes[3][:], x_rows[:, 3, :])
+        wv_raw = keep.tile([P, PACK, N], F32, name="wv_raw")
+        nc.sync.dma_start(wv_raw[:], wv.rearrange("(p i) n -> p i n", i=PACK))
+        bias = keep.tile([P, PACK], F32, name="bias")
+        nc.sync.dma_start(bias[:], bg.rearrange("(p t) -> p t", t=PACK))
+        res_rows = res.rearrange("(p t) j -> p t j", t=PACK)
+        carried = []
+        for c in range(CHUNKS):
+            tile = keep.tile([P, PACK, C], F32, name="carried%d" % c)
+            nc.sync.dma_start(tile[:], res_rows[:, :, c * C : (c + 1) * C])
+            carried.append(tile)
+
+        wk_codes = keep.tile([P, 2 * N], U8, name="wk_codes", align_bytes=64)
+        nc.vector.tensor_copy(
+            wk_codes[:].rearrange("p (t m b) -> p t m b", t=PACK, b=2),
+            wk_raw[:].rearrange("p (m t b) -> p t m b", t=PACK, b=2),
+        )
+        wk_plane = keep.tile([P, N], U8, name="wk_plane", align_bytes=64)
+        nc.vector.tensor_copy(
+            wk_plane[:].rearrange("p (t m) -> p t m", t=PACK),
+            wk_scale_raw[:].rearrange("p (m t) -> p t m", t=PACK),
+        )
+
+        picked = keep.tile([P, PACK, J], F32, name="picked")
+
+        def gather(i, j0, j1):
+            nc.vector.tensor_tensor(
+                picked[:, i, j0:j1], planes[i][:].indirect(offsets[:, j0 // 16 : j1 // 16]), weights[:, j0:j1], ALU.mult
+            )
+
+        gather(0, 0, J // 2)
+        gather(0, J // 2, J)
+        gather(1, 0, J)
+        gather(2, 0, J)
+
+        wv_codes = keep.tile([P, N], U32, name="wv_codes", align_bytes=64)
+        wv_plane = keep.tile([P, N], U8, name="wv_plane", align_bytes=64)
+        out_rows = out_0.rearrange("(p t) j -> p t j", t=PACK)
+        out_words = out_1[0].rearrange("p j i -> p (j i)")
+        y_plane = keep.tile([P, J], U8, name="y_plane", align_bytes=64)
+
+        def interleave(copy, dst, src):
+            copy(
+                dst.rearrange("p (c e t) -> p c t e", e=4, t=PACK),
+                src.rearrange("p t (c e) -> p c t e", e=4),
+            )
+
+        x_bf, x_codes, x_plane = [], [], []
+        for c in range(CHUNKS):
+            gather(3, c * C, (c + 1) * C)
+            tile = keep.tile([P, C * PACK], BF16, name="x_bf%d" % c, align_bytes=64)
+            interleave(nc.scalar.copy, tile[:], picked[:, :, c * C : (c + 1) * C])
+            x_bf.append(tile)
+
+        def quantise_x(c):
+            codes = keep.tile([P, C], U32, name="x_codes%d" % c, align_bytes=64)
+            plane = keep.tile([P, C], U8, name="x_plane%d" % c, align_bytes=64)
+            nc.vector.quantize_mx(out=codes[:].bitcast(FP8X4), scales=plane[:], in_=x_bf[c][:])
+            x_codes.append(codes)
+            x_plane.append(plane)
+
+        banks = {}
+        gates = {}
+
+        def products(c):
+            gate = keep.tile([P, PACK, C], F32, name="gate%d" % c)
+            ke = [psum.tile([P, 2, C], F32, name="ke%d" % h) for h in range(2)]
+            ve = [psum.tile([P, 2, C], F32, name="ve%d" % h) for h in range(2)]
+            for t in range(PACK):
+                nc.tensor.matmul_mx(
+                    out=ke[t // 2][:, t % 2, :],
+                    lhsT=wk_codes[:, 2 * P * t : 2 * P * (t + 1)].bitcast(FP4X4),
+                    lhsT_scale=wk_plane[:, P * t : P * (t + 1)],
+                    rhs=x_codes[c][:].bitcast(FP8X4),
+                    rhs_scale=x_plane[c][:],
+                    start=True,
+                    stop=True,
+                )
+            for t in range(PACK):
+                nc.tensor.matmul_mx(
+                    out=ve[t // 2][:, t % 2, :],
+                    lhsT=wv_codes[:, P * t : P * (t + 1)].bitcast(FP8X4),
+                    lhsT_scale=wv_plane[:, P * t : P * (t + 1)],
+                    rhs=x_codes[c][:].bitcast(FP8X4),
+                    rhs_scale=x_plane[c][:],
+                    start=True,
+                    stop=True,
+                )
+            for t in range(PACK):
+                nc.scalar.activation(gate[:, t, :], ke[t // 2][:, t % 2, :], ACT.Sigmoid, bias=bias[:, t : t + 1])
+            banks[c] = ve
+            gates[c] = gate
+
+        pieces = []
+
+        def finish(c, step, a, b, copy):
+            name = "%d_%d" % (c, a)
+            y = keep.tile([P, PACK, b - a], F32, name="y" + name)
+            parts = [slice(0, 2), slice(2, 4)] if b - a == C else [slice(0, 4)]
+            for rows in parts:
+                nc.vector.tensor_tensor(y[:, rows, :], step[:, rows, a:b], carried[c][:, rows, a:b], ALU.add)
+            nc.sync.dma_start(out_rows[:, :, c * C + a : c * C + b], y[:])
+            return (name, y, c * C + a, c * C + b, copy)
+
+        def round_y(piece):
+            name, y, j0, j1, copy = piece
+            tile = keep.tile([P, (j1 - j0) * PACK], BF16, name="y_bf" + name, align_bytes=64)
+            interleave(copy, tile[:], y[:])
+            return (name, tile, j0, j1)
+
+        def highway(c):
+            step = keep.tile([P, PACK, C], F32, name="step%d" % c)
+            halves = [slice(0, 2), slice(2, 4)]
+            for h in range(2):
+                nc.vector.scalar_tensor_tensor(step[:, halves[h], :], banks[c][h][:], 0.0, carried[c][:, halves[h], :], ALU.max, ALU.subtract)
+            for h in range(2):
+                nc.vector.tensor_tensor(step[:, halves[h], :], step[:, halves[h], :], gates[c][:, halves[h], :], ALU.mult)
+            return step
+
+        def hand_on(piece):
+            name, tile, j0, j1 = piece
+            codes = keep.tile([P, j1 - j0], U32, name="y_codes" + name, align_bytes=64)
+            nc.vector.quantize_mx(out=codes[:].bitcast(FP8X4), scales=y_plane[:, j0:j1], in_=tile[:])
+            nc.sync.dma_start(out_words[:, PACK * j0 : PACK * j1].bitcast(I32), codes[:].bitcast(I32))
+
+        quantise_x(0)
+        wv_bf = keep.tile([P, N * PACK], BF16, name="wv_bf", align_bytes=64)
+        nc.vector.tensor_copy(
+            wv_bf[:].rearrange("p (t m i) -> p m i t", t=PACK, i=PACK),
+            wv_raw[:].rearrange("p i (m t) -> p m i t", t=PACK),
+        )
+        quantise_x(1)
+        nc.vector.quantize_mx(out=wv_codes[:].bitcast(FP8X4), scales=wv_plane[:], in_=wv_bf[:])
+        products(0)
+        quantise_x(2)
+        products(1)
+        waiting = None
+        for c in range(CHUNKS - 1):
+            step = highway(c)
+            piece = round_y(finish(c, step, 0, C, nc.scalar.copy))
+            if c == 0:
+                quantise_x(3)
+            if c + 2 < CHUNKS:
+                products(c + 2)
+            if waiting:
+                hand_on(waiting)
+            waiting = piece
+        step = highway(CHUNKS - 1)
+        first = round_y(finish(CHUNKS - 1, step, 0, C // 2, nc.scalar.copy))
+        last = finish(CHUNKS - 1, step, C // 2, C, nc.vector.tensor_copy)
+        hand_on(waiting)
+        last = round_y(last)
+        hand_on(first)
+        hand_on(last)
+        for q in range(4):
+            queue = nc.scalar if q % 2 else nc.sync
+            queue.dma_start(out_2[0, 4 * q : 4 * q + 4, :].bitcast(I32), y_plane[32 * q : 32 * q + 4, :].bitcast(I32))

@@ -20,6 +20,7 @@ P = 128
 PACK = 4
 C = 256
 CHUNKS = J // C
+CUT = 640
 
 
 def tile_list_hwayreluP_kernel(tc, xT, wgt, wk_words, wk_scales, wv, bg, res, offs, out_0, out_1, out_2):
@@ -90,6 +91,7 @@ def tile_list_hwayreluP_kernel(tc, xT, wgt, wk_words, wk_scales, wv, bg, res, of
         wv_plane = keep.tile([P, N], U8, name="wv_plane", align_bytes=64)
         out_rows = out_0.rearrange("(p t) j -> p t j", t=PACK)
         out_words = out_1[0].rearrange("p j i -> p (j i)")
+        y_codes = keep.tile([P, J], U32, name="y_codes", align_bytes=64)
         y_plane = keep.tile([P, J], U8, name="y_plane", align_bytes=64)
 
         def interleave(copy, dst, src):
@@ -99,11 +101,16 @@ def tile_list_hwayreluP_kernel(tc, xT, wgt, wk_words, wk_scales, wv, bg, res, of
             )
 
         x_bf, x_codes, x_plane = [], [], []
-        for c in range(CHUNKS):
-            gather(3, c * C, (c + 1) * C)
+
+        def round_x(c):
             tile = keep.tile([P, C * PACK], BF16, name="x_bf%d" % c, align_bytes=64)
             interleave(nc.scalar.copy, tile[:], picked[:, :, c * C : (c + 1) * C])
             x_bf.append(tile)
+
+        for c in range(CHUNKS):
+            gather(3, c * C, (c + 1) * C)
+        round_x(0)
+        round_x(1)
 
         def quantise_x(c):
             codes = keep.tile([P, C], U32, name="x_codes%d" % c, align_bytes=64)
@@ -144,37 +151,41 @@ def tile_list_hwayreluP_kernel(tc, xT, wgt, wk_words, wk_scales, wv, bg, res, of
             banks[c] = ve
             gates[c] = gate
 
-        pieces = []
+        flat = "p t j -> p (t j)"
+        halves = [slice(0, 2), slice(2, 4)]
 
-        def finish(c, step, a, b, copy):
-            name = "%d_%d" % (c, a)
-            y = keep.tile([P, PACK, b - a], F32, name="y" + name)
-            parts = [slice(0, 2), slice(2, 4)] if b - a == C else [slice(0, 4)]
-            for rows in parts:
-                nc.vector.tensor_tensor(y[:, rows, :], step[:, rows, a:b], carried[c][:, rows, a:b], ALU.add)
-            nc.sync.dma_start(out_rows[:, :, c * C + a : c * C + b], y[:])
-            return (name, y, c * C + a, c * C + b, copy)
-
-        def round_y(piece):
-            name, y, j0, j1, copy = piece
-            tile = keep.tile([P, (j1 - j0) * PACK], BF16, name="y_bf" + name, align_bytes=64)
-            interleave(copy, tile[:], y[:])
-            return (name, tile, j0, j1)
-
-        def highway(c):
+        def difference(c):
             step = keep.tile([P, PACK, C], F32, name="step%d" % c)
-            halves = [slice(0, 2), slice(2, 4)]
             for h in range(2):
                 nc.vector.scalar_tensor_tensor(step[:, halves[h], :], banks[c][h][:], 0.0, carried[c][:, halves[h], :], ALU.max, ALU.subtract)
-            for h in range(2):
-                nc.vector.tensor_tensor(step[:, halves[h], :], step[:, halves[h], :], gates[c][:, halves[h], :], ALU.mult)
             return step
+
+        def gated(c, step, cut):
+            values, gate = step[:].rearrange(flat), gates[c][:].rearrange(flat)
+            for part in (slice(0, cut), slice(cut, PACK * C)):
+                nc.vector.tensor_tensor(values[:, part], values[:, part], gate[:, part], ALU.mult)
+
+        def round_y(name, y, j0, j1, copy):
+            tile = keep.tile([P, (j1 - j0) * PACK], BF16, name="y_bf" + name, align_bytes=64)
+            interleave(copy, tile[:], y)
+            return (name, tile, j0, j1)
+
+        def finish_shared(c, step):
+            y = keep.tile([P, PACK, C], F32, name="y%d" % c)
+            for engine, part in ((nc.vector, slice(0, CUT)), (nc.gpsimd, slice(CUT, PACK * C))):
+                engine.tensor_tensor(y[:].rearrange(flat)[:, part], step[:].rearrange(flat)[:, part], carried[c][:].rearrange(flat)[:, part], ALU.add)
+            nc.sync.dma_start(out_rows[:, :, c * C : (c + 1) * C], y[:])
+            return y
+
+        def finish_part(c, step, y, a, b):
+            nc.vector.tensor_tensor(y[:, :, a:b], step[:, :, a:b], carried[c][:, :, a:b], ALU.add)
 
         def hand_on(piece):
             name, tile, j0, j1 = piece
-            codes = keep.tile([P, j1 - j0], U32, name="y_codes" + name, align_bytes=64)
-            nc.vector.quantize_mx(out=codes[:].bitcast(FP8X4), scales=y_plane[:, j0:j1], in_=tile[:])
-            nc.sync.dma_start(out_words[:, PACK * j0 : PACK * j1].bitcast(I32), codes[:].bitcast(I32))
+            nc.vector.quantize_mx(out=y_codes[:, j0:j1].bitcast(FP8X4), scales=y_plane[:, j0:j1], in_=tile[:])
+
+        def store_words(j0, j1):
+            nc.sync.dma_start(out_words[:, PACK * j0 : PACK * j1].bitcast(I32), y_codes[:, j0:j1].bitcast(I32))
 
         quantise_x(0)
         wv_bf = keep.tile([P, N * PACK], BF16, name="wv_bf", align_bytes=64)
@@ -184,27 +195,40 @@ def tile_list_hwayreluP_kernel(tc, xT, wgt, wk_words, wk_scales, wv, bg, res, of
         )
         quantise_x(1)
         nc.vector.quantize_mx(out=wv_codes[:].bitcast(FP8X4), scales=wv_plane[:], in_=wv_bf[:])
+        round_x(2)
         products(0)
         quantise_x(2)
+        round_x(3)
         products(1)
-        waiting = None
+        rounded = []
         for c in range(CHUNKS - 1):
-            step = highway(c)
-            piece = round_y(finish(c, step, 0, C, nc.scalar.copy))
+            step = difference(c)
             if c == 0:
                 quantise_x(3)
+            if c == 2:
+                hand_on(rounded[0])
+                store_words(0, C)
             if c + 2 < CHUNKS:
                 products(c + 2)
-            if waiting:
-                hand_on(waiting)
-            waiting = piece
-        step = highway(CHUNKS - 1)
-        first = round_y(finish(CHUNKS - 1, step, 0, C // 2, nc.scalar.copy))
-        last = finish(CHUNKS - 1, step, C // 2, C, nc.vector.tensor_copy)
-        hand_on(waiting)
-        last = round_y(last)
+            gated(c, step, CUT)
+            y = finish_shared(c, step)
+            rounded.append(round_y(str(c), y[:], c * C, (c + 1) * C, nc.scalar.copy))
+        c = CHUNKS - 1
+        step = difference(c)
+        gated(c, step, PACK * C // 2)
+        hand_on(rounded[1])
+        y = keep.tile([P, PACK, C], F32, name="y%d" % c)
+        finish_part(c, step, y, 0, C // 2)
+        nc.sync.dma_start(out_rows[:, :, c * C : c * C + C // 2], y[:, :, : C // 2])
+        first = round_y("first", y[:, :, : C // 2], c * C, c * C + C // 2, nc.scalar.copy)
+        finish_part(c, step, y, C // 2, C)
+        nc.sync.dma_start(out_rows[:, :, c * C + C // 2 :], y[:, :, C // 2 :])
+        hand_on(rounded[2])
+        store_words(C, c * C)
+        last = round_y("last", y[:, :, C // 2 :], c * C + C // 2, J, nc.vector.tensor_copy)
         hand_on(first)
         hand_on(last)
+        store_words(c * C, J)
         for q in range(4):
             queue = nc.scalar if q % 2 else nc.sync
             queue.dma_start(out_2[0, 4 * q : 4 * q + 4, :].bitcast(I32), y_plane[32 * q : 32 * q + 4, :].bitcast(I32))

@@ -20,7 +20,7 @@ P = 128
 PACK = 4
 C = 256
 CHUNKS = J // C
-CUT = 640
+SLOT_PAIRS = (slice(0, 2), slice(2, 4))
 
 
 def tile_list_hwayreluP_kernel(tc, xT, wgt, wk_words, wk_scales, wv, bg, res, offs, out_0, out_1, out_2):
@@ -31,38 +31,29 @@ def tile_list_hwayreluP_kernel(tc, xT, wgt, wk_words, wk_scales, wv, bg, res, of
 
         offsets = keep.tile([P, J // 16], U16, name="offsets")
         nc.sync.dma_start(offsets[:], offs)
-
-        wk_scale_raw = keep.tile([P, N], U8, name="wk_scale_raw", align_bytes=64)
-        nc.vector.memset(wk_scale_raw[:].bitcast(U32), 0)
-
         wk_raw = keep.tile([P, 2 * N], U8, name="wk_raw", align_bytes=64)
         nc.sync.dma_start(wk_raw[:].bitcast(I32), wk_words[0].bitcast(I32))
+        wk_scales_raw = keep.tile([P, N], U8, name="wk_scales_raw", align_bytes=64)
+        nc.vector.memset(wk_scales_raw[:].bitcast(U32), 0)
         for q in range(4):
-            nc.scalar.dma_start(wk_scale_raw[32 * q : 32 * q + 4, :].bitcast(I32), wk_scales[0, 4 * q : 4 * q + 4, :].bitcast(I32))
-        warm = keep.tile([P, 1], F32, name="warm")
-        warm2 = keep.tile([P, 1], F32, name="warm2")
-        nc.vector.memset(warm[:], 0.0)
-        nc.scalar.activation(warm2[:], warm[:], ACT.Sigmoid)
+            nc.scalar.dma_start(wk_scales_raw[32 * q : 32 * q + 4, :].bitcast(I32), wk_scales[0, 4 * q : 4 * q + 4, :].bitcast(I32))
 
         weights = keep.tile([P, J], F32, name="weights")
         x_rows = xT.rearrange("(p i) t -> p i t", i=PACK)
-        planes = [keep.tile([P, T], F32, name="plane%d" % i) for i in range(PACK)]
+        tokens = [keep.tile([P, T], F32, name="tokens%d" % i) for i in range(PACK)]
+        bias = keep.tile([P, PACK], F32, name="bias")
         nc.sync.dma_start(weights[:, : J // 2], wgt[:, : J // 2])
-        nc.sync.dma_start(planes[0][:], x_rows[:, 0, :])
+        nc.sync.dma_start(tokens[0][:], x_rows[:, 0, :])
         nc.sync.dma_start(weights[:, J // 2 :], wgt[:, J // 2 :])
-        nc.sync.dma_start(planes[1][:], x_rows[:, 1, :])
-        nc.sync.dma_start(planes[2][:], x_rows[:, 2, :])
-        nc.sync.dma_start(planes[3][:], x_rows[:, 3, :])
+        for i in range(1, PACK):
+            nc.sync.dma_start(tokens[i][:], x_rows[:, i, :])
+        nc.sync.dma_start(bias[:], bg.rearrange("(p t) -> p t", t=PACK))
         wv_raw = keep.tile([P, PACK, N], F32, name="wv_raw")
         nc.sync.dma_start(wv_raw[:], wv.rearrange("(p i) n -> p i n", i=PACK))
-        bias = keep.tile([P, PACK], F32, name="bias")
-        nc.sync.dma_start(bias[:], bg.rearrange("(p t) -> p t", t=PACK))
         res_rows = res.rearrange("(p t) j -> p t j", t=PACK)
-        carried = []
+        carried = [keep.tile([P, PACK, C], F32, name="carried%d" % c) for c in range(CHUNKS)]
         for c in range(CHUNKS):
-            tile = keep.tile([P, PACK, C], F32, name="carried%d" % c)
-            nc.sync.dma_start(tile[:], res_rows[:, :, c * C : (c + 1) * C])
-            carried.append(tile)
+            nc.sync.dma_start(carried[c][:], res_rows[:, :, c * C : (c + 1) * C])
 
         wk_codes = keep.tile([P, 2 * N], U8, name="wk_codes", align_bytes=64)
         nc.vector.tensor_copy(
@@ -72,27 +63,15 @@ def tile_list_hwayreluP_kernel(tc, xT, wgt, wk_words, wk_scales, wv, bg, res, of
         wk_plane = keep.tile([P, N], U8, name="wk_plane", align_bytes=64)
         nc.vector.tensor_copy(
             wk_plane[:].rearrange("p (t m) -> p t m", t=PACK),
-            wk_scale_raw[:].rearrange("p (m t) -> p t m", t=PACK),
+            wk_scales_raw[:].rearrange("p (m t) -> p t m", t=PACK),
         )
 
         picked = keep.tile([P, PACK, J], F32, name="picked")
 
         def gather(i, j0, j1):
             nc.vector.tensor_tensor(
-                picked[:, i, j0:j1], planes[i][:].indirect(offsets[:, j0 // 16 : j1 // 16]), weights[:, j0:j1], ALU.mult
+                picked[:, i, j0:j1], tokens[i][:].indirect(offsets[:, j0 // 16 : j1 // 16]), weights[:, j0:j1], ALU.mult
             )
-
-        gather(0, 0, J // 2)
-        gather(0, J // 2, J)
-        gather(1, 0, J)
-        gather(2, 0, J)
-
-        wv_codes = keep.tile([P, N], U32, name="wv_codes", align_bytes=64)
-        wv_plane = keep.tile([P, N], U8, name="wv_plane", align_bytes=64)
-        out_rows = out_0.rearrange("(p t) j -> p t j", t=PACK)
-        out_words = out_1[0].rearrange("p j i -> p (j i)")
-        y_codes = keep.tile([P, J], U32, name="y_codes", align_bytes=64)
-        y_plane = keep.tile([P, J], U8, name="y_plane", align_bytes=64)
 
         def interleave(copy, dst, src):
             copy(
@@ -100,32 +79,37 @@ def tile_list_hwayreluP_kernel(tc, xT, wgt, wk_words, wk_scales, wv, bg, res, of
                 src.rearrange("p t (c e) -> p c t e", e=4),
             )
 
-        x_bf, x_codes, x_plane = [], [], []
+        x_bf = [keep.tile([P, C * PACK], BF16, name="x_bf%d" % c, align_bytes=64) for c in range(CHUNKS)]
+        x_codes = [keep.tile([P, C], U32, name="x_codes%d" % c, align_bytes=64) for c in range(CHUNKS)]
+        x_plane = [keep.tile([P, C], U8, name="x_plane%d" % c, align_bytes=64) for c in range(CHUNKS)]
 
         def round_x(c):
-            tile = keep.tile([P, C * PACK], BF16, name="x_bf%d" % c, align_bytes=64)
-            interleave(nc.scalar.copy, tile[:], picked[:, :, c * C : (c + 1) * C])
-            x_bf.append(tile)
-
-        for c in range(CHUNKS):
-            gather(3, c * C, (c + 1) * C)
-        round_x(0)
-        round_x(1)
+            interleave(nc.scalar.copy, x_bf[c][:], picked[:, :, c * C : (c + 1) * C])
 
         def quantise_x(c):
-            codes = keep.tile([P, C], U32, name="x_codes%d" % c, align_bytes=64)
-            plane = keep.tile([P, C], U8, name="x_plane%d" % c, align_bytes=64)
-            nc.vector.quantize_mx(out=codes[:].bitcast(FP8X4), scales=plane[:], in_=x_bf[c][:])
-            x_codes.append(codes)
-            x_plane.append(plane)
+            nc.vector.quantize_mx(out=x_codes[c][:].bitcast(FP8X4), scales=x_plane[c][:], in_=x_bf[c][:])
 
-        banks = {}
-        gates = {}
+        wv_bf = [keep.tile([P, 2 * P * PACK], BF16, name="wv_bf%d" % h, align_bytes=64) for h in range(2)]
+        wv_codes = [keep.tile([P, 2 * P], U32, name="wv_codes%d" % h, align_bytes=64) for h in range(2)]
+        wv_plane = [keep.tile([P, 2 * P], U8, name="wv_plane%d" % h, align_bytes=64) for h in range(2)]
 
-        def products(c):
-            gate = keep.tile([P, PACK, C], F32, name="gate%d" % c)
+        def round_wv(h):
+            nc.vector.tensor_copy(
+                wv_bf[h][:].rearrange("p (t m i) -> p m i t", t=2, i=PACK),
+                wv_raw[:].rearrange("p i (m t) -> p m i t", t=PACK)[:, :, :, SLOT_PAIRS[h]],
+            )
+
+        def quantise_wv(h):
+            nc.vector.quantize_mx(out=wv_codes[h][:].bitcast(FP8X4), scales=wv_plane[h][:], in_=wv_bf[h][:])
+
+        half_bias = keep.tile([P, PACK], F32, name="half_bias")
+        swing = [keep.tile([P, PACK, C], F32, name="swing%d" % c) for c in range(CHUNKS)]
+        step = [keep.tile([P, PACK, C], F32, name="step%d" % c) for c in range(CHUNKS)]
+        y = [keep.tile([P, PACK, C], F32, name="y%d" % c) for c in range(CHUNKS)]
+        value_banks = {}
+
+        def gate_products(c):
             ke = [psum.tile([P, 2, C], F32, name="ke%d" % h) for h in range(2)]
-            ve = [psum.tile([P, 2, C], F32, name="ve%d" % h) for h in range(2)]
             for t in range(PACK):
                 nc.tensor.matmul_mx(
                     out=ke[t // 2][:, t % 2, :],
@@ -137,98 +121,108 @@ def tile_list_hwayreluP_kernel(tc, xT, wgt, wk_words, wk_scales, wv, bg, res, of
                     stop=True,
                 )
             for t in range(PACK):
+                nc.scalar.activation(swing[c][:, t, :], ke[t // 2][:, t % 2, :], ACT.Tanh, bias=half_bias[:, t : t + 1], scale=0.5)
+
+        def value_products(c):
+            value_banks[c] = [psum.tile([P, 2, C], F32, name="ve%d" % h) for h in range(2)]
+            for t in range(PACK):
+                columns = slice(P * (t % 2), P * (t % 2 + 1))
                 nc.tensor.matmul_mx(
-                    out=ve[t // 2][:, t % 2, :],
-                    lhsT=wv_codes[:, P * t : P * (t + 1)].bitcast(FP8X4),
-                    lhsT_scale=wv_plane[:, P * t : P * (t + 1)],
+                    out=value_banks[c][t // 2][:, t % 2, :],
+                    lhsT=wv_codes[t // 2][:, columns].bitcast(FP8X4),
+                    lhsT_scale=wv_plane[t // 2][:, columns],
                     rhs=x_codes[c][:].bitcast(FP8X4),
                     rhs_scale=x_plane[c][:],
                     start=True,
                     stop=True,
                 )
-            for t in range(PACK):
-                nc.scalar.activation(gate[:, t, :], ke[t // 2][:, t % 2, :], ACT.Sigmoid, bias=bias[:, t : t + 1])
-            banks[c] = ve
-            gates[c] = gate
 
-        flat = "p t j -> p (t j)"
-        halves = [slice(0, 2), slice(2, 4)]
-
-        def difference(c):
-            step = keep.tile([P, PACK, C], F32, name="step%d" % c)
+        def subtract_carried(c):
             for h in range(2):
-                nc.vector.scalar_tensor_tensor(step[:, halves[h], :], banks[c][h][:], 0.0, carried[c][:, halves[h], :], ALU.max, ALU.subtract)
-            return step
+                rows = SLOT_PAIRS[h]
+                nc.vector.scalar_tensor_tensor(step[c][:, rows, :], value_banks[c][h][:], 0.0, carried[c][:, rows, :], ALU.max, ALU.subtract)
 
-        def gated(c, step, cut):
-            values, gate = step[:].rearrange(flat), gates[c][:].rearrange(flat)
-            for part in (slice(0, cut), slice(cut, PACK * C)):
-                nc.vector.tensor_tensor(values[:, part], values[:, part], gate[:, part], ALU.mult)
+        def apply_gate(c, rows, cols):
+            nc.vector.scalar_tensor_tensor(step[c][:, rows, cols], swing[c][:, rows, cols], 1.0, step[c][:, rows, cols], ALU.add, ALU.mult)
 
-        def round_y(name, y, j0, j1, copy):
-            tile = keep.tile([P, (j1 - j0) * PACK], BF16, name="y_bf" + name, align_bytes=64)
-            interleave(copy, tile[:], y)
-            return (name, tile, j0, j1)
+        def add_carried(c, rows, cols):
+            nc.vector.scalar_tensor_tensor(y[c][:, rows, cols], step[c][:, rows, cols], 0.5, carried[c][:, rows, cols], ALU.mult, ALU.add)
 
-        def finish_shared(c, step):
-            y = keep.tile([P, PACK, C], F32, name="y%d" % c)
-            for engine, part in ((nc.vector, slice(0, CUT)), (nc.gpsimd, slice(CUT, PACK * C))):
-                engine.tensor_tensor(y[:].rearrange(flat)[:, part], step[:].rearrange(flat)[:, part], carried[c][:].rearrange(flat)[:, part], ALU.add)
-            nc.sync.dma_start(out_rows[:, :, c * C : (c + 1) * C], y[:])
-            return y
+        out_rows = out_0.rearrange("(p t) j -> p t j", t=PACK)
+        out_words = out_1[0].rearrange("p j i -> p (j i)")
+        y_bf = keep.tile([P, J * PACK], BF16, name="y_bf", align_bytes=64)
+        y_codes = keep.tile([P, J], U32, name="y_codes", align_bytes=64)
+        y_plane = keep.tile([P, J], U8, name="y_plane", align_bytes=64)
 
-        def finish_part(c, step, y, a, b):
-            nc.vector.tensor_tensor(y[:, :, a:b], step[:, :, a:b], carried[c][:, :, a:b], ALU.add)
+        def store_y(c, a, b):
+            nc.sync.dma_start(out_rows[:, :, c * C + a : c * C + b], y[c][:, :, a:b])
 
-        def hand_on(piece):
-            name, tile, j0, j1 = piece
-            nc.vector.quantize_mx(out=y_codes[:, j0:j1].bitcast(FP8X4), scales=y_plane[:, j0:j1], in_=tile[:])
+        def round_y(copy, c, a, b):
+            interleave(copy, y_bf[:, PACK * (c * C + a) : PACK * (c * C + b)], y[c][:, :, a:b])
+
+        def quantise_y(j0, j1):
+            nc.vector.quantize_mx(out=y_codes[:, j0:j1].bitcast(FP8X4), scales=y_plane[:, j0:j1], in_=y_bf[:, PACK * j0 : PACK * j1])
 
         def store_words(j0, j1):
             nc.sync.dma_start(out_words[:, PACK * j0 : PACK * j1].bitcast(I32), y_codes[:, j0:j1].bitcast(I32))
 
+        gather(0, 0, J // 2)
+        gather(0, J // 2, J)
+        gather(1, 0, J)
+        gather(2, 0, J)
+        gather(3, 0, C)
+        gather(3, C, 2 * C)
+        gather(3, 2 * C, J)
+        round_x(0)
+        nc.scalar.mul(half_bias[:], bias[:], 0.5)
+        round_x(1)
         quantise_x(0)
-        wv_bf = keep.tile([P, N * PACK], BF16, name="wv_bf", align_bytes=64)
-        nc.vector.tensor_copy(
-            wv_bf[:].rearrange("p (t m i) -> p m i t", t=PACK, i=PACK),
-            wv_raw[:].rearrange("p i (m t) -> p m i t", t=PACK),
-        )
+        gate_products(0)
+        round_wv(0)
+        round_wv(1)
+        quantise_wv(0)
+        quantise_wv(1)
+        value_products(0)
         quantise_x(1)
-        nc.vector.quantize_mx(out=wv_codes[:].bitcast(FP8X4), scales=wv_plane[:], in_=wv_bf[:])
-        round_x(2)
-        products(0)
-        quantise_x(2)
-        round_x(3)
-        products(1)
-        rounded = []
-        for c in range(CHUNKS - 1):
-            step = difference(c)
-            if c == 0:
-                quantise_x(3)
-            if c == 2:
-                hand_on(rounded[0])
-                store_words(0, C)
+
+        whole = slice(0, C)
+        last = CHUNKS - 1
+        for c in range(last):
             if c + 2 < CHUNKS:
-                products(c + 2)
-            gated(c, step, CUT)
-            y = finish_shared(c, step)
-            rounded.append(round_y(str(c), y[:], c * C, (c + 1) * C, nc.scalar.copy))
-        c = CHUNKS - 1
-        step = difference(c)
-        gated(c, step, PACK * C // 2)
-        hand_on(rounded[1])
-        y = keep.tile([P, PACK, C], F32, name="y%d" % c)
-        finish_part(c, step, y, 0, C // 2)
-        nc.sync.dma_start(out_rows[:, :, c * C : c * C + C // 2], y[:, :, : C // 2])
-        first = round_y("first", y[:, :, : C // 2], c * C, c * C + C // 2, nc.scalar.copy)
-        finish_part(c, step, y, C // 2, C)
-        nc.sync.dma_start(out_rows[:, :, c * C + C // 2 :], y[:, :, C // 2 :])
-        hand_on(rounded[2])
-        store_words(C, c * C)
-        last = round_y("last", y[:, :, C // 2 :], c * C + C // 2, J, nc.vector.tensor_copy)
-        hand_on(first)
-        hand_on(last)
-        store_words(c * C, J)
+                round_x(c + 2)
+            gate_products(c + 1)
+            value_products(c + 1)
+            subtract_carried(c)
+            for rows in SLOT_PAIRS:
+                apply_gate(c, rows, whole)
+            for rows in SLOT_PAIRS:
+                add_carried(c, rows, whole)
+            store_y(c, 0, C)
+            round_y(nc.scalar.copy, c, 0, C)
+            if c + 2 < CHUNKS:
+                quantise_x(c + 2)
+            if c == 1:
+                quantise_y(0, C)
+                store_words(0, C)
+
+        every = slice(0, PACK)
+        half = C // 2
+        subtract_carried(last)
+        quantise_y(C, 2 * C)
+        store_words(C, 2 * C)
+        apply_gate(last, every, slice(0, half))
+        apply_gate(last, every, slice(half, C))
+        add_carried(last, every, slice(0, half))
+        store_y(last, 0, half)
+        round_y(nc.scalar.copy, last, 0, half)
+        add_carried(last, every, slice(half, C))
+        store_y(last, half, C)
+        quantise_y(2 * C, 3 * C)
+        store_words(2 * C, 3 * C)
+        round_y(nc.vector.tensor_copy, last, half, C)
+        quantise_y(last * C, last * C + half)
+        quantise_y(last * C + half, J)
+        store_words(last * C, J)
         for q in range(4):
             queue = nc.scalar if q % 2 else nc.sync
             queue.dma_start(out_2[0, 4 * q : 4 * q + 4, :].bitcast(I32), y_plane[32 * q : 32 * q + 4, :].bitcast(I32))

@@ -103,14 +103,15 @@ def tile_list_hwayreluP_kernel(tc, xT, wgt, wk_words, wk_scales, wv, bg, res, of
             nc.vector.quantize_mx(out=wv_codes[h][:].bitcast(FP8X4), scales=wv_plane[h][:], in_=wv_bf[h][:])
 
         half_bias = keep.tile([P, PACK], F32, name="half_bias")
-        swing = [keep.tile([P, PACK, C], F32, name="swing%d" % c) for c in range(CHUNKS)]
-        step = [keep.tile([P, PACK, C], F32, name="step%d" % c) for c in range(CHUNKS)]
+        swing = [keep.tile([P, PACK, C], F32, name="swing%d" % c, tag="shared%d" % c) for c in range(CHUNKS)]
+        step = {}
         y = [keep.tile([P, PACK, C], F32, name="y%d" % c) for c in range(CHUNKS)]
         value_banks = {}
+        lower, upper = SLOT_PAIRS
 
         def gate_products(c):
             ke = [psum.tile([P, 2, C], F32, name="ke%d" % h) for h in range(2)]
-            for t in range(PACK):
+            for t in (2, 3, 0, 1):
                 nc.tensor.matmul_mx(
                     out=ke[t // 2][:, t % 2, :],
                     lhsT=wk_codes[:, 2 * P * t : 2 * P * (t + 1)].bitcast(FP4X4),
@@ -120,8 +121,10 @@ def tile_list_hwayreluP_kernel(tc, xT, wgt, wk_words, wk_scales, wv, bg, res, of
                     start=True,
                     stop=True,
                 )
-            for t in range(PACK):
+            for t in (2, 3, 0, 1):
                 nc.scalar.activation(swing[c][:, t, :], ke[t // 2][:, t % 2, :], ACT.Tanh, bias=half_bias[:, t : t + 1], scale=0.5)
+            if c < CHUNKS - 1:
+                nc.scalar.activation(swing[c][:, upper, :], swing[c][:, upper, :], ACT.Copy, bias=0.5, scale=0.5)
 
         def value_products(c):
             value_banks[c] = [psum.tile([P, 2, C], F32, name="ve%d" % h) for h in range(2)]
@@ -138,6 +141,7 @@ def tile_list_hwayreluP_kernel(tc, xT, wgt, wk_words, wk_scales, wv, bg, res, of
                 )
 
         def subtract_carried(c):
+            step[c] = keep.tile([P, PACK, C], F32, name="step%d" % c, tag="shared%d" % (c - 1) if c else "first_step")
             for h in range(2):
                 rows = SLOT_PAIRS[h]
                 nc.vector.scalar_tensor_tensor(step[c][:, rows, :], value_banks[c][h][:], 0.0, carried[c][:, rows, :], ALU.max, ALU.subtract)
@@ -176,6 +180,7 @@ def tile_list_hwayreluP_kernel(tc, xT, wgt, wk_words, wk_scales, wv, bg, res, of
         round_x(0)
         nc.scalar.mul(half_bias[:], bias[:], 0.5)
         round_x(1)
+        round_x(2)
         quantise_x(0)
         gate_products(0)
         round_wv(0)
@@ -188,28 +193,27 @@ def tile_list_hwayreluP_kernel(tc, xT, wgt, wk_words, wk_scales, wv, bg, res, of
         whole = slice(0, C)
         last = CHUNKS - 1
         for c in range(last):
-            if c + 2 < CHUNKS:
-                round_x(c + 2)
+            if c == 0:
+                round_x(3)
             gate_products(c + 1)
             value_products(c + 1)
             subtract_carried(c)
-            for rows in SLOT_PAIRS:
-                apply_gate(c, rows, whole)
-            for rows in SLOT_PAIRS:
-                add_carried(c, rows, whole)
-            store_y(c, 0, C)
-            round_y(nc.scalar.copy, c, 0, C)
+            apply_gate(c, lower, whole)
             if c + 2 < CHUNKS:
                 quantise_x(c + 2)
-            if c == 1:
+            else:
                 quantise_y(0, C)
                 store_words(0, C)
+            nc.vector.tensor_tensor(step[c][:, upper, :], step[c][:, upper, :], swing[c][:, upper, :], ALU.mult)
+            add_carried(c, lower, whole)
+            nc.gpsimd.tensor_tensor(y[c][:, upper, :], step[c][:, upper, :], carried[c][:, upper, :], ALU.add)
+            store_y(c, 0, C)
+            round_y(nc.scalar.copy, c, 0, C)
 
         every = slice(0, PACK)
         half = C // 2
         subtract_carried(last)
         quantise_y(C, 2 * C)
-        store_words(C, 2 * C)
         apply_gate(last, every, slice(0, half))
         apply_gate(last, every, slice(half, C))
         add_carried(last, every, slice(0, half))
@@ -218,7 +222,7 @@ def tile_list_hwayreluP_kernel(tc, xT, wgt, wk_words, wk_scales, wv, bg, res, of
         add_carried(last, every, slice(half, C))
         store_y(last, half, C)
         quantise_y(2 * C, 3 * C)
-        store_words(2 * C, 3 * C)
+        store_words(C, 3 * C)
         round_y(nc.vector.tensor_copy, last, half, C)
         quantise_y(last * C, last * C + half)
         quantise_y(last * C + half, J)

@@ -17,10 +17,15 @@ ALU = mybir.AluOpType
 ACT = mybir.ActivationFunctionType
 
 P = 128
-PACK = 4
+SLOTS = 4
+LIST_ROWS = 16
+QUADRANTS = 4
+RUN = 4
 C = 256
 CHUNKS = J // C
-SLOT_PAIRS = (slice(0, 2), slice(2, 4))
+LAST = CHUNKS - 1
+LOWER, UPPER = slice(0, 2), slice(2, 4)
+PAIRS = (LOWER, UPPER)
 
 
 def tile_list_hwayreluP_kernel(tc, xT, wgt, wk_words, wk_scales, wv, bg, res, offs, out_0, out_1, out_2):
@@ -29,59 +34,59 @@ def tile_list_hwayreluP_kernel(tc, xT, wgt, wk_words, wk_scales, wv, bg, res, of
         keep = ctx.enter_context(tc.tile_pool(name="keep", bufs=1))
         psum = ctx.enter_context(tc.psum_pool(name="psum", bufs=2))
 
-        offsets = keep.tile([P, J // 16], U16, name="offsets")
+        offsets = keep.tile([P, J // LIST_ROWS], U16, name="offsets")
         nc.sync.dma_start(offsets[:], offs)
         wk_raw = keep.tile([P, 2 * N], U8, name="wk_raw", align_bytes=64)
         nc.sync.dma_start(wk_raw[:].bitcast(I32), wk_words[0].bitcast(I32))
-        wk_scales_raw = keep.tile([P, N], U8, name="wk_scales_raw", align_bytes=64)
-        nc.vector.memset(wk_scales_raw[:].bitcast(U32), 0)
-        for q in range(4):
-            nc.scalar.dma_start(wk_scales_raw[32 * q : 32 * q + 4, :].bitcast(I32), wk_scales[0, 4 * q : 4 * q + 4, :].bitcast(I32))
+        wk_plane_raw = keep.tile([P, N], U8, name="wk_plane_raw", align_bytes=64)
+        nc.vector.memset(wk_plane_raw[:].bitcast(U32), 0)
+        for q in range(QUADRANTS):
+            nc.scalar.dma_start(
+                wk_plane_raw[32 * q : 32 * q + 4, :].bitcast(I32), wk_scales[0, 4 * q : 4 * q + 4, :].bitcast(I32)
+            )
 
-        weights = keep.tile([P, J], F32, name="weights")
-        x_rows = xT.rearrange("(p i) t -> p i t", i=PACK)
-        tokens = [keep.tile([P, T], F32, name="tokens%d" % i) for i in range(PACK)]
-        bias = keep.tile([P, PACK], F32, name="bias")
-        nc.sync.dma_start(weights[:, : J // 2], wgt[:, : J // 2])
+        pick_weights = keep.tile([P, J], F32, name="pick_weights")
+        x_rows = xT.rearrange("(p i) t -> p i t", i=SLOTS)
+        tokens = [keep.tile([P, T], F32, name="tokens%d" % i) for i in range(SLOTS)]
+        bias = keep.tile([P, SLOTS], F32, name="bias")
+        nc.sync.dma_start(pick_weights[:, : J // 2], wgt[:, : J // 2])
         nc.sync.dma_start(tokens[0][:], x_rows[:, 0, :])
-        nc.sync.dma_start(weights[:, J // 2 :], wgt[:, J // 2 :])
-        for i in range(1, PACK):
+        nc.sync.dma_start(pick_weights[:, J // 2 :], wgt[:, J // 2 :])
+        for i in range(1, SLOTS):
             nc.sync.dma_start(tokens[i][:], x_rows[:, i, :])
-        nc.sync.dma_start(bias[:], bg.rearrange("(p t) -> p t", t=PACK))
-        wv_raw = keep.tile([P, PACK, N], F32, name="wv_raw")
-        nc.sync.dma_start(wv_raw[:], wv.rearrange("(p i) n -> p i n", i=PACK))
-        res_rows = res.rearrange("(p t) j -> p t j", t=PACK)
-        carried = [keep.tile([P, PACK, C], F32, name="carried%d" % c) for c in range(CHUNKS)]
+        nc.sync.dma_start(bias[:], bg.rearrange("(p t) -> p t", t=SLOTS))
+        wv_raw = keep.tile([P, SLOTS, N], F32, name="wv_raw")
+        nc.sync.dma_start(wv_raw[:], wv.rearrange("(p i) n -> p i n", i=SLOTS))
+        res_rows = res.rearrange("(p t) j -> p t j", t=SLOTS)
+        carried = [keep.tile([P, SLOTS, C], F32, name="carried%d" % c) for c in range(CHUNKS)]
         for c in range(CHUNKS):
             nc.sync.dma_start(carried[c][:], res_rows[:, :, c * C : (c + 1) * C])
 
         wk_codes = keep.tile([P, 2 * N], U8, name="wk_codes", align_bytes=64)
         nc.vector.tensor_copy(
-            wk_codes[:].rearrange("p (t m b) -> p t m b", t=PACK, b=2),
-            wk_raw[:].rearrange("p (m t b) -> p t m b", t=PACK, b=2),
+            wk_codes[:].rearrange("p (t m b) -> p t m b", t=SLOTS, b=2),
+            wk_raw[:].rearrange("p (m t b) -> p t m b", t=SLOTS, b=2),
         )
         wk_plane = keep.tile([P, N], U8, name="wk_plane", align_bytes=64)
         nc.vector.tensor_copy(
-            wk_plane[:].rearrange("p (t m) -> p t m", t=PACK),
-            wk_scales_raw[:].rearrange("p (m t) -> p t m", t=PACK),
+            wk_plane[:].rearrange("p (t m) -> p t m", t=SLOTS),
+            wk_plane_raw[:].rearrange("p (m t) -> p t m", t=SLOTS),
         )
 
-        picked = keep.tile([P, PACK, J], F32, name="picked")
+        picked = keep.tile([P, SLOTS, J], F32, name="picked")
+        x_bf = [keep.tile([P, C * SLOTS], BF16, name="x_bf%d" % c, align_bytes=64) for c in range(CHUNKS)]
+        x_codes = [keep.tile([P, C], U32, name="x_codes%d" % c, align_bytes=64) for c in range(CHUNKS)]
+        x_plane = [keep.tile([P, C], U8, name="x_plane%d" % c, align_bytes=64) for c in range(CHUNKS)]
 
         def gather(i, j0, j1):
-            nc.vector.tensor_tensor(
-                picked[:, i, j0:j1], tokens[i][:].indirect(offsets[:, j0 // 16 : j1 // 16]), weights[:, j0:j1], ALU.mult
-            )
+            window = tokens[i][:].indirect(offsets[:, j0 // LIST_ROWS : j1 // LIST_ROWS])
+            nc.vector.tensor_tensor(picked[:, i, j0:j1], window, pick_weights[:, j0:j1], ALU.mult)
 
         def interleave(copy, dst, src):
             copy(
-                dst.rearrange("p (c e t) -> p c t e", e=4, t=PACK),
-                src.rearrange("p t (c e) -> p c t e", e=4),
+                dst.rearrange("p (c e t) -> p c t e", e=RUN, t=SLOTS),
+                src.rearrange("p t (c e) -> p c t e", e=RUN),
             )
-
-        x_bf = [keep.tile([P, C * PACK], BF16, name="x_bf%d" % c, align_bytes=64) for c in range(CHUNKS)]
-        x_codes = [keep.tile([P, C], U32, name="x_codes%d" % c, align_bytes=64) for c in range(CHUNKS)]
-        x_plane = [keep.tile([P, C], U8, name="x_plane%d" % c, align_bytes=64) for c in range(CHUNKS)]
 
         def round_x(c):
             interleave(nc.scalar.copy, x_bf[c][:], picked[:, :, c * C : (c + 1) * C])
@@ -89,29 +94,29 @@ def tile_list_hwayreluP_kernel(tc, xT, wgt, wk_words, wk_scales, wv, bg, res, of
         def quantise_x(c):
             nc.vector.quantize_mx(out=x_codes[c][:].bitcast(FP8X4), scales=x_plane[c][:], in_=x_bf[c][:])
 
-        wv_bf = [keep.tile([P, 2 * P * PACK], BF16, name="wv_bf%d" % h, align_bytes=64) for h in range(2)]
+        wv_bf = [keep.tile([P, 2 * P * SLOTS], BF16, name="wv_bf%d" % h, align_bytes=64) for h in range(2)]
         wv_codes = [keep.tile([P, 2 * P], U32, name="wv_codes%d" % h, align_bytes=64) for h in range(2)]
         wv_plane = [keep.tile([P, 2 * P], U8, name="wv_plane%d" % h, align_bytes=64) for h in range(2)]
 
         def round_wv(h):
             nc.vector.tensor_copy(
-                wv_bf[h][:].rearrange("p (t m i) -> p m i t", t=2, i=PACK),
-                wv_raw[:].rearrange("p i (m t) -> p m i t", t=PACK)[:, :, :, SLOT_PAIRS[h]],
+                wv_bf[h][:].rearrange("p (u m i) -> p m i u", u=2, i=SLOTS),
+                wv_raw[:].rearrange("p i (m t) -> p m i t", t=SLOTS)[:, :, :, PAIRS[h]],
             )
 
         def quantise_wv(h):
             nc.vector.quantize_mx(out=wv_codes[h][:].bitcast(FP8X4), scales=wv_plane[h][:], in_=wv_bf[h][:])
 
-        half_bias = keep.tile([P, PACK], F32, name="half_bias")
-        swing = [keep.tile([P, PACK, C], F32, name="swing%d" % c, tag="shared%d" % c) for c in range(CHUNKS)]
+        half_bias = keep.tile([P, SLOTS], F32, name="half_bias")
+        swing = [keep.tile([P, SLOTS, C], F32, name="swing%d" % c, tag="shared%d" % c) for c in range(CHUNKS)]
         step = {}
-        y = [keep.tile([P, PACK, C], F32, name="y%d" % c) for c in range(CHUNKS)]
+        y = [keep.tile([P, SLOTS, C], F32, name="y%d" % c) for c in range(CHUNKS)]
         value_banks = {}
-        lower, upper = SLOT_PAIRS
 
         def gate_products(c):
             ke = [psum.tile([P, 2, C], F32, name="ke%d" % h) for h in range(2)]
-            for t in (2, 3, 0, 1):
+            upper_first = (2, 3, 0, 1)
+            for t in upper_first:
                 nc.tensor.matmul_mx(
                     out=ke[t // 2][:, t % 2, :],
                     lhsT=wk_codes[:, 2 * P * t : 2 * P * (t + 1)].bitcast(FP4X4),
@@ -121,14 +126,16 @@ def tile_list_hwayreluP_kernel(tc, xT, wgt, wk_words, wk_scales, wv, bg, res, of
                     start=True,
                     stop=True,
                 )
-            for t in (2, 3, 0, 1):
-                nc.scalar.activation(swing[c][:, t, :], ke[t // 2][:, t % 2, :], ACT.Tanh, bias=half_bias[:, t : t + 1], scale=0.5)
-            if c < CHUNKS - 1:
-                nc.scalar.activation(swing[c][:, upper, :], swing[c][:, upper, :], ACT.Copy, bias=0.5, scale=0.5)
+            for t in upper_first:
+                nc.scalar.activation(
+                    swing[c][:, t, :], ke[t // 2][:, t % 2, :], ACT.Tanh, bias=half_bias[:, t : t + 1], scale=0.5
+                )
+            if c < LAST:
+                nc.scalar.activation(swing[c][:, UPPER, :], swing[c][:, UPPER, :], ACT.Copy, bias=0.5, scale=0.5)
 
         def value_products(c):
             value_banks[c] = [psum.tile([P, 2, C], F32, name="ve%d" % h) for h in range(2)]
-            for t in range(PACK):
+            for t in range(SLOTS):
                 columns = slice(P * (t % 2), P * (t % 2 + 1))
                 nc.tensor.matmul_mx(
                     out=value_banks[c][t // 2][:, t % 2, :],
@@ -141,34 +148,46 @@ def tile_list_hwayreluP_kernel(tc, xT, wgt, wk_words, wk_scales, wv, bg, res, of
                 )
 
         def subtract_carried(c):
-            step[c] = keep.tile([P, PACK, C], F32, name="step%d" % c, tag="shared%d" % (c - 1) if c else "first_step")
+            tag = "shared%d" % (c - 1) if c else "first_step"
+            step[c] = keep.tile([P, SLOTS, C], F32, name="step%d" % c, tag=tag)
             for h in range(2):
-                rows = SLOT_PAIRS[h]
-                nc.vector.scalar_tensor_tensor(step[c][:, rows, :], value_banks[c][h][:], 0.0, carried[c][:, rows, :], ALU.max, ALU.subtract)
+                nc.vector.scalar_tensor_tensor(
+                    step[c][:, PAIRS[h], :], value_banks[c][h][:], 0.0, carried[c][:, PAIRS[h], :], ALU.max, ALU.subtract
+                )
 
-        def apply_gate(c, rows, cols):
-            nc.vector.scalar_tensor_tensor(step[c][:, rows, cols], swing[c][:, rows, cols], 1.0, step[c][:, rows, cols], ALU.add, ALU.mult)
+        def apply_swing(c, slots, cols):
+            nc.vector.scalar_tensor_tensor(
+                step[c][:, slots, cols], swing[c][:, slots, cols], 1.0, step[c][:, slots, cols], ALU.add, ALU.mult
+            )
 
-        def add_carried(c, rows, cols):
-            nc.vector.scalar_tensor_tensor(y[c][:, rows, cols], step[c][:, rows, cols], 0.5, carried[c][:, rows, cols], ALU.mult, ALU.add)
+        def add_carried(c, slots, cols):
+            nc.vector.scalar_tensor_tensor(
+                y[c][:, slots, cols], step[c][:, slots, cols], 0.5, carried[c][:, slots, cols], ALU.mult, ALU.add
+            )
 
-        out_rows = out_0.rearrange("(p t) j -> p t j", t=PACK)
+        out_rows = out_0.rearrange("(p t) j -> p t j", t=SLOTS)
         out_words = out_1[0].rearrange("p j i -> p (j i)")
-        y_bf = keep.tile([P, J * PACK], BF16, name="y_bf", align_bytes=64)
+        y_bf = keep.tile([P, J * SLOTS], BF16, name="y_bf", align_bytes=64)
         y_codes = keep.tile([P, J], U32, name="y_codes", align_bytes=64)
         y_plane = keep.tile([P, J], U8, name="y_plane", align_bytes=64)
 
-        def store_y(c, a, b):
-            nc.sync.dma_start(out_rows[:, :, c * C + a : c * C + b], y[c][:, :, a:b])
+        def store_y(c, cols):
+            nc.sync.dma_start(out_rows[:, :, c * C + cols.start : c * C + cols.stop], y[c][:, :, cols])
 
-        def round_y(copy, c, a, b):
-            interleave(copy, y_bf[:, PACK * (c * C + a) : PACK * (c * C + b)], y[c][:, :, a:b])
+        def round_y(copy, c, cols):
+            interleave(copy, y_bf[:, SLOTS * (c * C + cols.start) : SLOTS * (c * C + cols.stop)], y[c][:, :, cols])
 
-        def quantise_y(j0, j1):
-            nc.vector.quantize_mx(out=y_codes[:, j0:j1].bitcast(FP8X4), scales=y_plane[:, j0:j1], in_=y_bf[:, PACK * j0 : PACK * j1])
+        def quantise_y(c, cols):
+            j0, j1 = c * C + cols.start, c * C + cols.stop
+            nc.vector.quantize_mx(
+                out=y_codes[:, j0:j1].bitcast(FP8X4), scales=y_plane[:, j0:j1], in_=y_bf[:, SLOTS * j0 : SLOTS * j1]
+            )
 
-        def store_words(j0, j1):
-            nc.sync.dma_start(out_words[:, PACK * j0 : PACK * j1].bitcast(I32), y_codes[:, j0:j1].bitcast(I32))
+        def store_words(c):
+            nc.sync.dma_start(
+                out_words[:, SLOTS * c * C : SLOTS * (c + 1) * C].bitcast(I32),
+                y_codes[:, c * C : (c + 1) * C].bitcast(I32),
+            )
 
         gather(0, 0, J // 2)
         gather(0, J // 2, J)
@@ -189,44 +208,43 @@ def tile_list_hwayreluP_kernel(tc, xT, wgt, wk_words, wk_scales, wv, bg, res, of
         quantise_wv(1)
         value_products(0)
         quantise_x(1)
+        round_x(LAST)
 
         whole = slice(0, C)
-        last = CHUNKS - 1
-        for c in range(last):
-            if c == 0:
-                round_x(3)
+        for c in range(LAST):
             gate_products(c + 1)
             value_products(c + 1)
             subtract_carried(c)
-            apply_gate(c, lower, whole)
+            apply_swing(c, LOWER, whole)
             if c + 2 < CHUNKS:
                 quantise_x(c + 2)
             else:
-                quantise_y(0, C)
-                store_words(0, C)
-            nc.vector.tensor_tensor(step[c][:, upper, :], step[c][:, upper, :], swing[c][:, upper, :], ALU.mult)
-            add_carried(c, lower, whole)
-            nc.gpsimd.tensor_tensor(y[c][:, upper, :], step[c][:, upper, :], carried[c][:, upper, :], ALU.add)
-            store_y(c, 0, C)
-            round_y(nc.scalar.copy, c, 0, C)
+                quantise_y(0, whole)
+                store_words(0)
+            nc.vector.tensor_tensor(step[c][:, UPPER, :], step[c][:, UPPER, :], swing[c][:, UPPER, :], ALU.mult)
+            add_carried(c, LOWER, whole)
+            nc.gpsimd.tensor_tensor(y[c][:, UPPER, :], step[c][:, UPPER, :], carried[c][:, UPPER, :], ALU.add)
+            store_y(c, whole)
+            round_y(nc.scalar.copy, c, whole)
 
-        every = slice(0, PACK)
-        half = C // 2
-        subtract_carried(last)
-        quantise_y(C, 2 * C)
-        apply_gate(last, every, slice(0, half))
-        apply_gate(last, every, slice(half, C))
-        add_carried(last, every, slice(0, half))
-        store_y(last, 0, half)
-        round_y(nc.scalar.copy, last, 0, half)
-        add_carried(last, every, slice(half, C))
-        store_y(last, half, C)
-        quantise_y(2 * C, 3 * C)
-        store_words(C, 3 * C)
-        round_y(nc.vector.tensor_copy, last, half, C)
-        quantise_y(last * C, last * C + half)
-        quantise_y(last * C + half, J)
-        store_words(last * C, J)
-        for q in range(4):
+        every = slice(0, SLOTS)
+        first, second = slice(0, C // 2), slice(C // 2, C)
+        subtract_carried(LAST)
+        quantise_y(1, whole)
+        store_words(1)
+        apply_swing(LAST, every, first)
+        apply_swing(LAST, every, second)
+        add_carried(LAST, every, first)
+        store_y(LAST, first)
+        round_y(nc.scalar.copy, LAST, first)
+        add_carried(LAST, every, second)
+        store_y(LAST, second)
+        quantise_y(2, whole)
+        store_words(2)
+        round_y(nc.vector.tensor_copy, LAST, second)
+        quantise_y(LAST, first)
+        quantise_y(LAST, second)
+        store_words(LAST)
+        for q in range(QUADRANTS):
             queue = nc.scalar if q % 2 else nc.sync
             queue.dma_start(out_2[0, 4 * q : 4 * q + 4, :].bitcast(I32), y_plane[32 * q : 32 * q + 4, :].bitcast(I32))

@@ -33,9 +33,13 @@ def tile_list_hwayreluP_kernel(tc, xT, wgt, wk_words, wk_scales, wv, bg, res, of
     with ExitStack() as ctx:
         keep = ctx.enter_context(tc.tile_pool(name="keep", bufs=1))
         psum = ctx.enter_context(tc.psum_pool(name="psum", bufs=2))
+        gate_psum = ctx.enter_context(tc.psum_pool(name="gate_psum", bufs=1))
+        after_wv = ctx.enter_context(tc.tile_pool(name="after_wv", bufs=1))
 
         offsets = keep.tile([P, J // LIST_ROWS], U16, name="offsets")
         nc.sync.dma_start(offsets[:], offs)
+        weight_rows = keep.tile([P, J // LIST_ROWS], F32, name="weight_rows", align_bytes=64)
+        nc.sync.dma_start(weight_rows[:], wgt.rearrange("(g r) j -> g r j", r=LIST_ROWS)[:, 0, :])
         wk_raw = keep.tile([P, 2 * N], U8, name="wk_raw", align_bytes=64)
         nc.sync.dma_start(wk_raw[:].bitcast(I32), wk_words[0].bitcast(I32))
         wk_plane_raw = keep.tile([P, N], U8, name="wk_plane_raw", align_bytes=64)
@@ -45,37 +49,48 @@ def tile_list_hwayreluP_kernel(tc, xT, wgt, wk_words, wk_scales, wv, bg, res, of
                 wk_plane_raw[32 * q : 32 * q + 4, :].bitcast(I32), wk_scales[0, 4 * q : 4 * q + 4, :].bitcast(I32)
             )
 
-        pick_weights = keep.tile([P, J], F32, name="pick_weights")
+        pick_weights = keep.tile([P, J], F32, name="pick_weights", align_bytes=64)
         x_rows = xT.rearrange("(p i) t -> p i t", i=SLOTS)
-        tokens = [keep.tile([P, T], F32, name="tokens%d" % i) for i in range(SLOTS)]
+        tokens = [keep.tile([P, T], F32, name="tokens%d" % i, align_bytes=64) for i in range(SLOTS)]
         bias = keep.tile([P, SLOTS], F32, name="bias")
-        nc.sync.dma_start(pick_weights[:, : J // 2], wgt[:, : J // 2])
-        nc.sync.dma_start(tokens[0][:], x_rows[:, 0, :])
-        nc.sync.dma_start(pick_weights[:, J // 2 :], wgt[:, J // 2 :])
-        for i in range(1, SLOTS):
+        wv_raw = after_wv.tile([P, 2, SLOTS, N // 2], F32, name="wv_raw", align_bytes=64, offset=0)
+        wv_rows = wv.rearrange("(p i) (a n) -> p a i n", i=SLOTS, a=2)
+        for i in range(SLOTS - 1):
             nc.sync.dma_start(tokens[i][:], x_rows[:, i, :])
+        nc.sync.dma_start(wv_raw[:, 0], wv_rows[:, 0])
+        nc.sync.dma_start(tokens[SLOTS - 1][:], x_rows[:, SLOTS - 1, :])
+        nc.sync.dma_start(wv_raw[:, 1], wv_rows[:, 1])
         nc.sync.dma_start(bias[:], bg.rearrange("(p t) -> p t", t=SLOTS))
-        wv_raw = keep.tile([P, SLOTS, N], F32, name="wv_raw")
-        nc.sync.dma_start(wv_raw[:], wv.rearrange("(p i) n -> p i n", i=SLOTS))
         res_rows = res.rearrange("(p t) j -> p t j", t=SLOTS)
         carried = [keep.tile([P, SLOTS, C], F32, name="carried%d" % c) for c in range(CHUNKS)]
         for c in range(CHUNKS):
             nc.sync.dma_start(carried[c][:], res_rows[:, :, c * C : (c + 1) * C])
+
+        warm = keep.tile([P, 2], F32, name="warm")
+        nc.vector.memset(warm[:, 0:1], 0.0)
+        nc.scalar.activation(warm[:, 1:2], warm[:, 0:1], ACT.Sigmoid)
+
+        turned = keep.tile([P, 64], F32, name="turned", align_bytes=64)
+        for s in range(2):
+            nc.vector.transpose(turned[:, 32 * s : 32 * (s + 1)], weight_rows[:, 32 * s : 32 * (s + 1)])
+        repeated = keep.tile([P, J], F32, name="repeated", align_bytes=64)
+        for u in range(2):
+            half = slice(u * J // 2, (u + 1) * J // 2)
+            nc.scalar.copy(
+                repeated[:, half].rearrange("p (b q r) -> p b q r", q=4, r=LIST_ROWS),
+                turned[:].rearrange("p (q b) -> p b q", q=4)[:, 8 * u : 8 * (u + 1), :].unsqueeze(3).to_broadcast([P, 8, 4, LIST_ROWS]),
+            )
+            nc.vector.transpose(pick_weights[:, half], repeated[:, half])
 
         wk_codes = keep.tile([P, 2 * N], U8, name="wk_codes", align_bytes=64)
         nc.vector.tensor_copy(
             wk_codes[:].rearrange("p (t m b) -> p t m b", t=SLOTS, b=2),
             wk_raw[:].rearrange("p (m t b) -> p t m b", t=SLOTS, b=2),
         )
-        wk_plane = keep.tile([P, N], U8, name="wk_plane", align_bytes=64)
-        nc.vector.tensor_copy(
-            wk_plane[:].rearrange("p (t m) -> p t m", t=SLOTS),
-            wk_plane_raw[:].rearrange("p (m t) -> p t m", t=SLOTS),
-        )
 
         picked = keep.tile([P, SLOTS, J], F32, name="picked")
-        x_bf = [keep.tile([P, C * SLOTS], BF16, name="x_bf%d" % c, align_bytes=64) for c in range(CHUNKS)]
-        x_codes = [keep.tile([P, C], U32, name="x_codes%d" % c, align_bytes=64) for c in range(CHUNKS)]
+        x_bf = {c: keep.tile([P, C * SLOTS], BF16, name="x_bf%d" % c, align_bytes=64) for c in range(2)}
+        x_codes = {c: keep.tile([P, C], U32, name="x_codes%d" % c, align_bytes=64) for c in (0, 2, 3)}
         x_plane = [keep.tile([P, C], U8, name="x_plane%d" % c, align_bytes=64) for c in range(CHUNKS)]
 
         def gather(i, j0, j1):
@@ -91,6 +106,12 @@ def tile_list_hwayreluP_kernel(tc, xT, wgt, wk_words, wk_scales, wv, bg, res, of
         def round_x(c):
             interleave(nc.scalar.copy, x_bf[c][:], picked[:, :, c * C : (c + 1) * C])
 
+        def round_x_pair(c, slots):
+            nc.scalar.copy(
+                x_bf[c][:].rearrange("p (c e t) -> p c t e", e=RUN, t=SLOTS)[:, :, slots, :],
+                picked[:, slots, c * C : (c + 1) * C].rearrange("p t (c e) -> p c t e", e=RUN),
+            )
+
         def quantise_x(c):
             nc.vector.quantize_mx(out=x_codes[c][:].bitcast(FP8X4), scales=x_plane[c][:], in_=x_bf[c][:])
 
@@ -98,25 +119,23 @@ def tile_list_hwayreluP_kernel(tc, xT, wgt, wk_words, wk_scales, wv, bg, res, of
         wv_codes = [keep.tile([P, 2 * P], U32, name="wv_codes%d" % h, align_bytes=64) for h in range(2)]
         wv_plane = [keep.tile([P, 2 * P], U8, name="wv_plane%d" % h, align_bytes=64) for h in range(2)]
 
-        def round_wv(h):
-            nc.vector.tensor_copy(
-                wv_bf[h][:].rearrange("p (u m i) -> p m i u", u=2, i=SLOTS),
-                wv_raw[:].rearrange("p i (m t) -> p m i t", t=SLOTS)[:, :, :, PAIRS[h]],
+        def round_wv(a, h):
+            nc.scalar.copy(
+                wv_bf[h][:].rearrange("p (u m i) -> p m i u", u=2, i=SLOTS)[:, a * P // 2 : (a + 1) * P // 2],
+                wv_raw[:, a].rearrange("p i (m t) -> p m i t", t=SLOTS)[:, :, :, PAIRS[h]],
             )
 
         def quantise_wv(h):
             nc.vector.quantize_mx(out=wv_codes[h][:].bitcast(FP8X4), scales=wv_plane[h][:], in_=wv_bf[h][:])
 
-        half_bias = keep.tile([P, SLOTS], F32, name="half_bias")
-        swing = [keep.tile([P, SLOTS, C], F32, name="swing%d" % c, tag="shared%d" % c) for c in range(CHUNKS)]
+        gate = {c: keep.tile([P, SLOTS, C], F32, name="gate%d" % c, tag="shared%d" % c) for c in range(1, CHUNKS)}
         step = {}
         y = [keep.tile([P, SLOTS, C], F32, name="y%d" % c) for c in range(CHUNKS)]
         value_banks = {}
 
         def gate_products(c):
-            ke = [psum.tile([P, 2, C], F32, name="ke%d" % h) for h in range(2)]
-            upper_first = (2, 3, 0, 1)
-            for t in upper_first:
+            ke = [gate_psum.tile([P, 2, C], F32, name="ke%d" % h) for h in range(2)]
+            for t in range(SLOTS):
                 nc.tensor.matmul_mx(
                     out=ke[t // 2][:, t % 2, :],
                     lhsT=wk_codes[:, 2 * P * t : 2 * P * (t + 1)].bitcast(FP4X4),
@@ -126,12 +145,8 @@ def tile_list_hwayreluP_kernel(tc, xT, wgt, wk_words, wk_scales, wv, bg, res, of
                     start=True,
                     stop=True,
                 )
-            for t in upper_first:
-                nc.scalar.activation(
-                    swing[c][:, t, :], ke[t // 2][:, t % 2, :], ACT.Tanh, bias=half_bias[:, t : t + 1], scale=0.5
-                )
-            if c < LAST:
-                nc.scalar.activation(swing[c][:, UPPER, :], swing[c][:, UPPER, :], ACT.Copy, bias=0.5, scale=0.5)
+            for t in range(SLOTS):
+                nc.scalar.activation(gate[c][:, t, :], ke[t // 2][:, t % 2, :], ACT.Sigmoid, bias=bias[:, t : t + 1])
 
         def value_products(c):
             value_banks[c] = [psum.tile([P, 2, C], F32, name="ve%d" % h) for h in range(2)]
@@ -148,22 +163,21 @@ def tile_list_hwayreluP_kernel(tc, xT, wgt, wk_words, wk_scales, wv, bg, res, of
                 )
 
         def subtract_carried(c):
-            tag = "shared%d" % (c - 1) if c else "first_step"
-            step[c] = keep.tile([P, SLOTS, C], F32, name="step%d" % c, tag=tag)
+            if c == 1:
+                step[c] = after_wv.tile([P, SLOTS, C], F32, name="step1", align_bytes=64, offset=0)
+            else:
+                tag = "shared%d" % (c - 1) if c else "first_step"
+                step[c] = keep.tile([P, SLOTS, C], F32, name="step%d" % c, tag=tag)
             for h in range(2):
                 nc.vector.scalar_tensor_tensor(
                     step[c][:, PAIRS[h], :], value_banks[c][h][:], 0.0, carried[c][:, PAIRS[h], :], ALU.max, ALU.subtract
                 )
 
-        def apply_swing(c, slots, cols):
-            nc.vector.scalar_tensor_tensor(
-                step[c][:, slots, cols], swing[c][:, slots, cols], 1.0, step[c][:, slots, cols], ALU.add, ALU.mult
-            )
+        def apply_gate(c, slots, cols):
+            nc.vector.tensor_tensor(step[c][:, slots, cols], step[c][:, slots, cols], gate[c][:, slots, cols], ALU.mult)
 
-        def add_carried(c, slots, cols):
-            nc.vector.scalar_tensor_tensor(
-                y[c][:, slots, cols], step[c][:, slots, cols], 0.5, carried[c][:, slots, cols], ALU.mult, ALU.add
-            )
+        def add_carried(engine, c, slots, cols):
+            engine.tensor_tensor(y[c][:, slots, cols], step[c][:, slots, cols], carried[c][:, slots, cols], ALU.add)
 
         out_rows = out_0.rearrange("(p t) j -> p t j", t=SLOTS)
         out_words = out_1[0].rearrange("p j i -> p (j i)")
@@ -191,53 +205,68 @@ def tile_list_hwayreluP_kernel(tc, xT, wgt, wk_words, wk_scales, wv, bg, res, of
 
         gather(0, 0, J // 2)
         gather(0, J // 2, J)
-        gather(1, 0, J)
+        gather(1, 0, J // 2)
+        gather(1, J // 2, J)
+        round_x_pair(0, LOWER)
+        round_x_pair(1, LOWER)
         gather(2, 0, J)
+        wk_plane = keep.tile([P, N], U8, name="wk_plane", tag="tokens2", align_bytes=64)
+        nc.vector.tensor_copy(
+            wk_plane[:].rearrange("p (t m) -> p t m", t=SLOTS),
+            wk_plane_raw[:].rearrange("p (m t) -> p t m", t=SLOTS),
+        )
+        round_wv(0, 0)
+        round_wv(0, 1)
         gather(3, 0, C)
         gather(3, C, 2 * C)
         gather(3, 2 * C, J)
-        round_x(0)
-        nc.scalar.mul(half_bias[:], bias[:], 0.5)
-        round_x(1)
-        round_x(2)
+        round_x_pair(0, UPPER)
+        round_x_pair(1, UPPER)
         quantise_x(0)
+        round_wv(1, 0)
+        round_wv(1, 1)
+        gate[0] = after_wv.tile([P, SLOTS, C], F32, name="gate0", align_bytes=64, offset=0)
+        x_bf[2] = after_wv.tile([P, C * SLOTS], BF16, name="x_bf2", align_bytes=64, offset=4096)
+        round_x(2)
         gate_products(0)
-        round_wv(0)
-        round_wv(1)
         quantise_wv(0)
         quantise_wv(1)
-        value_products(0)
+        x_codes[1] = after_wv.tile([P, C], U32, name="x_codes1", align_bytes=64, offset=6144)
         quantise_x(1)
-        round_x(LAST)
+        value_products(0)
+        x_bf[3] = keep.tile([P, C * SLOTS], BF16, name="x_bf3", tag="x_bf1", align_bytes=64)
 
         whole = slice(0, C)
+        subtract_carried(0)
         for c in range(LAST):
             gate_products(c + 1)
             value_products(c + 1)
-            subtract_carried(c)
-            apply_swing(c, LOWER, whole)
-            if c + 2 < CHUNKS:
-                quantise_x(c + 2)
+            apply_gate(c, LOWER, whole)
+            if c == 0:
+                quantise_x(2)
+                round_x(3)
+            elif c == 1:
+                quantise_x(3)
             else:
                 quantise_y(0, whole)
                 store_words(0)
-            nc.vector.tensor_tensor(step[c][:, UPPER, :], step[c][:, UPPER, :], swing[c][:, UPPER, :], ALU.mult)
-            add_carried(c, LOWER, whole)
-            nc.gpsimd.tensor_tensor(y[c][:, UPPER, :], step[c][:, UPPER, :], carried[c][:, UPPER, :], ALU.add)
+            apply_gate(c, UPPER, whole)
+            add_carried(nc.vector, c, LOWER, whole)
+            add_carried(nc.gpsimd, c, UPPER, whole)
+            subtract_carried(c + 1)
             store_y(c, whole)
             round_y(nc.scalar.copy, c, whole)
 
         every = slice(0, SLOTS)
         first, second = slice(0, C // 2), slice(C // 2, C)
-        subtract_carried(LAST)
         quantise_y(1, whole)
         store_words(1)
-        apply_swing(LAST, every, first)
-        apply_swing(LAST, every, second)
-        add_carried(LAST, every, first)
+        apply_gate(LAST, every, first)
+        apply_gate(LAST, every, second)
+        add_carried(nc.vector, LAST, every, first)
         store_y(LAST, first)
         round_y(nc.scalar.copy, LAST, first)
-        add_carried(LAST, every, second)
+        add_carried(nc.vector, LAST, every, second)
         store_y(LAST, second)
         quantise_y(2, whole)
         store_words(2)

@@ -88,14 +88,23 @@ def tile_list_hwayreluP_kernel(tc, xT, wgt, wk_words, wk_scales, wv, bg, res, of
             wk_raw[:].rearrange("p (m t b) -> p t m b", t=SLOTS, b=2),
         )
 
-        picked = keep.tile([P, SLOTS, J], F32, name="picked")
+        early = keep.tile([P, 2, 2 * C], F32, name="early")
+        late = keep.tile([P, 11 * C], F32, name="late")
         x_bf = {c: keep.tile([P, C * SLOTS], BF16, name="x_bf%d" % c, align_bytes=64) for c in range(2)}
         x_codes = {c: keep.tile([P, C], U32, name="x_codes%d" % c, align_bytes=64) for c in (0, 2, 3)}
         x_plane = [keep.tile([P, C], U8, name="x_plane%d" % c, align_bytes=64) for c in range(CHUNKS)]
 
         def gather(i, j0, j1):
             window = tokens[i][:].indirect(offsets[:, j0 // LIST_ROWS : j1 // LIST_ROWS])
-            nc.vector.tensor_tensor(picked[:, i, j0:j1], window, pick_weights[:, j0:j1], ALU.mult)
+            if j0 >= 2 * C:
+                start = 2 * i * C + j0 - 2 * C
+                out = late[:, start : start + j1 - j0]
+            elif i < 2:
+                out = early[:, i, j0:j1]
+            else:
+                start = (5 + i) * C + 2 * j0
+                out = late[:, start : start + C]
+            nc.vector.tensor_tensor(out, window, pick_weights[:, j0:j1], ALU.mult)
 
         def interleave(copy, dst, src):
             copy(
@@ -104,23 +113,27 @@ def tile_list_hwayreluP_kernel(tc, xT, wgt, wk_words, wk_scales, wv, bg, res, of
             )
 
         def round_x(c):
-            interleave(nc.scalar.copy, x_bf[c][:], picked[:, :, c * C : (c + 1) * C])
+            interleave(nc.scalar.copy, x_bf[c][:], late[:, : 8 * C].rearrange("p (t c) -> p t c", t=SLOTS)[:, :, (c - 2) * C : (c - 1) * C])
 
         def round_x_pair(c, slots):
+            if slots == LOWER:
+                pair = early[:, :, c * C : (c + 1) * C]
+            else:
+                pair = late[:, (7 + 2 * c) * C : (9 + 2 * c) * C].rearrange("p (t c) -> p t c", t=2)
             nc.scalar.copy(
                 x_bf[c][:].rearrange("p (c e t) -> p c t e", e=RUN, t=SLOTS)[:, :, slots, :],
-                picked[:, slots, c * C : (c + 1) * C].rearrange("p t (c e) -> p c t e", e=RUN),
+                pair.rearrange("p t (c e) -> p c t e", e=RUN),
             )
 
         def quantise_x(c):
             nc.vector.quantize_mx(out=x_codes[c][:].bitcast(FP8X4), scales=x_plane[c][:], in_=x_bf[c][:])
 
         wv_bf = [keep.tile([P, 2 * P * SLOTS], BF16, name="wv_bf%d" % h, align_bytes=64) for h in range(2)]
-        wv_codes = [keep.tile([P, 2 * P], U32, name="wv_codes%d" % h, align_bytes=64) for h in range(2)]
+        wv_codes = {0: keep.tile([P, 2 * P], U32, name="wv_codes0", align_bytes=64)}
         wv_plane = [keep.tile([P, 2 * P], U8, name="wv_plane%d" % h, align_bytes=64) for h in range(2)]
 
-        def round_wv(a, h):
-            nc.scalar.copy(
+        def round_wv(copy, a, h):
+            copy(
                 wv_bf[h][:].rearrange("p (u m i) -> p m i u", u=2, i=SLOTS)[:, a * P // 2 : (a + 1) * P // 2],
                 wv_raw[:, a].rearrange("p i (m t) -> p m i t", t=SLOTS)[:, :, :, PAIRS[h]],
             )
@@ -132,12 +145,13 @@ def tile_list_hwayreluP_kernel(tc, xT, wgt, wk_words, wk_scales, wv, bg, res, of
         step = {}
         y = [keep.tile([P, SLOTS, C], F32, name="y%d" % c) for c in range(CHUNKS)]
         value_banks = {}
+        gate_banks = {}
 
-        def gate_products(c):
-            ke = [gate_psum.tile([P, 2, C], F32, name="ke%d" % h) for h in range(2)]
-            for t in range(SLOTS):
+        def gate_products(c, order):
+            gate_banks[c] = [gate_psum.tile([P, 2, C], F32, name="ke%d" % h) for h in range(2)]
+            for t in order:
                 nc.tensor.matmul_mx(
-                    out=ke[t // 2][:, t % 2, :],
+                    out=gate_banks[c][t // 2][:, t % 2, :],
                     lhsT=wk_codes[:, 2 * P * t : 2 * P * (t + 1)].bitcast(FP4X4),
                     lhsT_scale=wk_plane[:, P * t : P * (t + 1)],
                     rhs=x_codes[c][:].bitcast(FP8X4),
@@ -145,8 +159,12 @@ def tile_list_hwayreluP_kernel(tc, xT, wgt, wk_words, wk_scales, wv, bg, res, of
                     start=True,
                     stop=True,
                 )
-            for t in range(SLOTS):
-                nc.scalar.activation(gate[c][:, t, :], ke[t // 2][:, t % 2, :], ACT.Sigmoid, bias=bias[:, t : t + 1])
+
+        def open_gates(c, order):
+            for t in order:
+                nc.scalar.activation(
+                    gate[c][:, t, :], gate_banks[c][t // 2][:, t % 2, :], ACT.Sigmoid, bias=bias[:, t : t + 1]
+                )
 
         def value_products(c):
             value_banks[c] = [psum.tile([P, 2, C], F32, name="ve%d" % h) for h in range(2)]
@@ -166,8 +184,7 @@ def tile_list_hwayreluP_kernel(tc, xT, wgt, wk_words, wk_scales, wv, bg, res, of
             if c == 1:
                 step[c] = after_wv.tile([P, SLOTS, C], F32, name="step1", align_bytes=64, offset=0)
             else:
-                tag = "shared%d" % (c - 1) if c else "first_step"
-                step[c] = keep.tile([P, SLOTS, C], F32, name="step%d" % c, tag=tag)
+                step[c] = keep.tile([P, SLOTS, C], F32, name="step%d" % c, tag="shared%d" % (c - 1))
             for h in range(2):
                 nc.vector.scalar_tensor_tensor(
                     step[c][:, PAIRS[h], :], value_banks[c][h][:], 0.0, carried[c][:, PAIRS[h], :], ALU.max, ALU.subtract
@@ -209,45 +226,72 @@ def tile_list_hwayreluP_kernel(tc, xT, wgt, wk_words, wk_scales, wv, bg, res, of
         gather(1, J // 2, J)
         round_x_pair(0, LOWER)
         round_x_pair(1, LOWER)
-        gather(2, 0, J)
+        gather(2, 0, C)
+        gather(2, C, 2 * C)
+        gather(2, 2 * C, J)
         wk_plane = keep.tile([P, N], U8, name="wk_plane", tag="tokens2", align_bytes=64)
         nc.vector.tensor_copy(
             wk_plane[:].rearrange("p (t m) -> p t m", t=SLOTS),
             wk_plane_raw[:].rearrange("p (m t) -> p t m", t=SLOTS),
         )
-        round_wv(0, 0)
-        round_wv(0, 1)
+        round_wv(nc.scalar.copy, 0, 0)
+        round_wv(nc.scalar.copy, 0, 1)
         gather(3, 0, C)
         gather(3, C, 2 * C)
-        gather(3, 2 * C, J)
+        gather(3, 2 * C, 3 * C)
         round_x_pair(0, UPPER)
         round_x_pair(1, UPPER)
         quantise_x(0)
-        round_wv(1, 0)
-        round_wv(1, 1)
+        gather(3, 3 * C, J)
+        round_wv(nc.scalar.copy, 1, 0)
+        round_wv(nc.vector.tensor_copy, 1, 1)
         gate[0] = after_wv.tile([P, SLOTS, C], F32, name="gate0", align_bytes=64, offset=0)
-        x_bf[2] = after_wv.tile([P, C * SLOTS], BF16, name="x_bf2", align_bytes=64, offset=4096)
-        round_x(2)
-        gate_products(0)
+        carry_gate = after_wv.tile([P, 2, C], F32, name="carry_gate", align_bytes=64, offset=4096)
+        wv_codes[1] = after_wv.tile([P, 2 * P], U32, name="wv_codes1", align_bytes=64, offset=7168)
+        x_codes[1] = after_wv.tile([P, C], U32, name="x_codes1", align_bytes=64, offset=6144)
+        minus_bias = keep.tile([P, SLOTS], F32, name="minus_bias")
+        nc.scalar.mul(minus_bias[:], bias[:], -1.0)
+        gate_products(0, (2, 3, 0, 1))
+        for t in (2, 3):
+            nc.scalar.activation(
+                carry_gate[:, t - 2, :], gate_banks[0][1][:, t - 2, :], ACT.Sigmoid, bias=minus_bias[:, t : t + 1], scale=-1.0
+            )
+        open_gates(0, (2, 3, 0, 1))
         quantise_wv(0)
         quantise_wv(1)
-        x_codes[1] = after_wv.tile([P, C], U32, name="x_codes1", align_bytes=64, offset=6144)
         quantise_x(1)
         value_products(0)
+        x_bf[2] = keep.tile([P, C * SLOTS], BF16, name="x_bf2", tag="wv_bf0", align_bytes=64)
+        round_x(2)
         x_bf[3] = keep.tile([P, C * SLOTS], BF16, name="x_bf3", tag="x_bf1", align_bytes=64)
 
         whole = slice(0, C)
-        subtract_carried(0)
-        for c in range(LAST):
-            gate_products(c + 1)
+        kept = keep.tile([P, 2, C], F32, name="kept", tag="wv_bf1", align_bytes=64)
+        nc.gpsimd.tensor_tensor(kept[:], carry_gate[:], carried[0][:, UPPER, :], ALU.mult)
+        step[0] = keep.tile([P, SLOTS, C], F32, name="step0")
+        nc.vector.scalar_tensor_tensor(
+            step[0][:, LOWER, :], value_banks[0][0][:], 0.0, carried[0][:, LOWER, :], ALU.max, ALU.subtract
+        )
+        nc.vector.scalar_tensor_tensor(
+            step[0][:, UPPER, :], value_banks[0][1][:], 0.0, gate[0][:, UPPER, :], ALU.max, ALU.mult
+        )
+        value_products(1)
+        gate_products(1, range(SLOTS))
+        open_gates(1, range(SLOTS))
+        round_x(3)
+        apply_gate(0, LOWER, whole)
+        nc.vector.tensor_tensor(y[0][:, UPPER, :], step[0][:, UPPER, :], kept[:], ALU.add)
+        add_carried(nc.gpsimd, 0, LOWER, whole)
+        subtract_carried(1)
+        store_y(0, whole)
+        round_y(nc.scalar.copy, 0, whole)
+        for c in range(1, LAST):
+            quantise_x(c + 1)
             value_products(c + 1)
+            gate_products(c + 1, range(SLOTS))
+            open_gates(c + 1, range(SLOTS))
             apply_gate(c, LOWER, whole)
-            if c == 0:
-                quantise_x(2)
-                round_x(3)
-            elif c == 1:
-                quantise_x(3)
-            else:
+            if c == LAST - 1:
                 quantise_y(0, whole)
                 store_words(0)
             apply_gate(c, UPPER, whole)

@@ -74,9 +74,9 @@ def tile_list_hwayreluP_kernel(tc, xT, wgt, wk_words, wk_scales, wv, bg, res, of
         for s in range(2):
             nc.vector.transpose(turned[:, 32 * s : 32 * (s + 1)], weight_rows[:, 32 * s : 32 * (s + 1)])
         repeated = keep.tile([P, J], F32, name="repeated", align_bytes=64)
-        for u in range(2):
+        for u, copy in enumerate((nc.vector.tensor_copy, nc.scalar.copy)):
             half = slice(u * J // 2, (u + 1) * J // 2)
-            nc.scalar.copy(
+            copy(
                 repeated[:, half].rearrange("p (b q r) -> p b q r", q=4, r=LIST_ROWS),
                 turned[:].rearrange("p (q b) -> p b q", q=4)[:, 8 * u : 8 * (u + 1), :].unsqueeze(3).to_broadcast([P, 8, 4, LIST_ROWS]),
             )
@@ -121,8 +121,8 @@ def tile_list_hwayreluP_kernel(tc, xT, wgt, wk_words, wk_scales, wv, bg, res, of
             else:
                 pair = late[:, (7 + 2 * c) * C : (9 + 2 * c) * C].rearrange("p (t c) -> p t c", t=2)
             nc.scalar.copy(
-                x_bf[c][:].rearrange("p (c e t) -> p c t e", e=RUN, t=SLOTS)[:, :, slots, :],
-                pair.rearrange("p t (c e) -> p c t e", e=RUN),
+                x_bf[c][:].rearrange("p (c t) -> p c t", t=SLOTS)[:, :, slots],
+                pair.rearrange("p t c -> p c t"),
             )
 
         def quantise_x(c):

@@ -34,7 +34,6 @@ def tile_list_hwayreluP_kernel(tc, xT, wgt, wk_words, wk_scales, wv, bg, res, of
         keep = ctx.enter_context(tc.tile_pool(name="keep", bufs=1))
         psum = ctx.enter_context(tc.psum_pool(name="psum", bufs=2))
         gate_psum = ctx.enter_context(tc.psum_pool(name="gate_psum", bufs=1))
-        after_wv = ctx.enter_context(tc.tile_pool(name="after_wv", bufs=1))
 
         offsets = keep.tile([P, J // LIST_ROWS], U16, name="offsets")
         nc.sync.dma_start(offsets[:], offs)
@@ -53,14 +52,14 @@ def tile_list_hwayreluP_kernel(tc, xT, wgt, wk_words, wk_scales, wv, bg, res, of
         x_rows = xT.rearrange("(p i) t -> p i t", i=SLOTS)
         tokens = [keep.tile([P, T], F32, name="tokens%d" % i, align_bytes=64) for i in range(SLOTS)]
         bias = keep.tile([P, SLOTS], F32, name="bias")
-        wv_raw = after_wv.tile([P, 2, SLOTS, N // 2], F32, name="wv_raw", align_bytes=64, offset=0)
+        wv_raw = keep.tile([P, 2, SLOTS, N // 2], F32, name="wv_raw")
         wv_rows = wv.rearrange("(p i) (a n) -> p a i n", i=SLOTS, a=2)
         for i in range(SLOTS - 1):
             nc.sync.dma_start(tokens[i][:], x_rows[:, i, :])
         nc.sync.dma_start(wv_raw[:, 0], wv_rows[:, 0])
         nc.sync.dma_start(tokens[SLOTS - 1][:], x_rows[:, SLOTS - 1, :])
-        nc.sync.dma_start(wv_raw[:, 1], wv_rows[:, 1])
         nc.sync.dma_start(bias[:], bg.rearrange("(p t) -> p t", t=SLOTS))
+        nc.sync.dma_start(wv_raw[:, 1], wv_rows[:, 1])
         res_rows = res.rearrange("(p t) j -> p t j", t=SLOTS)
         carried = [keep.tile([P, SLOTS, C], F32, name="carried%d" % c) for c in range(CHUNKS)]
         for c in range(CHUNKS):
@@ -88,22 +87,20 @@ def tile_list_hwayreluP_kernel(tc, xT, wgt, wk_words, wk_scales, wv, bg, res, of
             wk_raw[:].rearrange("p (m t b) -> p t m b", t=SLOTS, b=2),
         )
 
-        early = keep.tile([P, 2, 2 * C], F32, name="early")
-        late = keep.tile([P, 11 * C], F32, name="late")
-        x_bf = {c: keep.tile([P, C * SLOTS], BF16, name="x_bf%d" % c, align_bytes=64) for c in range(2)}
-        x_codes = {c: keep.tile([P, C], U32, name="x_codes%d" % c, align_bytes=64) for c in (0, 2, 3)}
+        early = keep.tile([P, 2, J], F32, name="early")
+        late = keep.tile([P, 7, C], F32, name="late")
+        late_blocks = {0: (1, 4), 1: (2, 5), 2: (3, 6), 3: (0, 3)}
+        x_bf = [keep.tile([P, C * SLOTS], BF16, name="x_bf%d" % c, align_bytes=64) for c in range(CHUNKS)]
+        x_codes = {c: keep.tile([P, C], U32, name="x_codes%d" % c, align_bytes=64) for c in range(CHUNKS)}
         x_plane = [keep.tile([P, C], U8, name="x_plane%d" % c, align_bytes=64) for c in range(CHUNKS)]
 
         def gather(i, j0, j1):
             window = tokens[i][:].indirect(offsets[:, j0 // LIST_ROWS : j1 // LIST_ROWS])
-            if j0 >= 2 * C:
-                start = 2 * i * C + j0 - 2 * C
-                out = late[:, start : start + j1 - j0]
-            elif i < 2:
+            if i < 2:
                 out = early[:, i, j0:j1]
             else:
-                start = (5 + i) * C + 2 * j0
-                out = late[:, start : start + C]
+                block = late_blocks[j0 // C][i - 2]
+                out = late[:, block : block + (j1 - j0) // C, :].rearrange("p b c -> p (b c)")
             nc.vector.tensor_tensor(out, window, pick_weights[:, j0:j1], ALU.mult)
 
         def interleave(copy, dst, src):
@@ -112,14 +109,11 @@ def tile_list_hwayreluP_kernel(tc, xT, wgt, wk_words, wk_scales, wv, bg, res, of
                 src.rearrange("p t (c e) -> p c t e", e=RUN),
             )
 
-        def round_x(c):
-            interleave(nc.scalar.copy, x_bf[c][:], late[:, : 8 * C].rearrange("p (t c) -> p t c", t=SLOTS)[:, :, (c - 2) * C : (c - 1) * C])
-
         def round_x_pair(c, slots):
             if slots == LOWER:
                 pair = early[:, :, c * C : (c + 1) * C]
             else:
-                pair = late[:, (7 + 2 * c) * C : (9 + 2 * c) * C].rearrange("p (t c) -> p t c", t=2)
+                pair = late[:, late_blocks[c][0] : late_blocks[c][1] + 1 : 3, :]
             nc.scalar.copy(
                 x_bf[c][:].rearrange("p (c t) -> p c t", t=SLOTS)[:, :, slots],
                 pair.rearrange("p t c -> p c t"),
@@ -129,7 +123,7 @@ def tile_list_hwayreluP_kernel(tc, xT, wgt, wk_words, wk_scales, wv, bg, res, of
             nc.vector.quantize_mx(out=x_codes[c][:].bitcast(FP8X4), scales=x_plane[c][:], in_=x_bf[c][:])
 
         wv_bf = [keep.tile([P, 2 * P * SLOTS], BF16, name="wv_bf%d" % h, align_bytes=64) for h in range(2)]
-        wv_codes = {0: keep.tile([P, 2 * P], U32, name="wv_codes0", align_bytes=64)}
+        wv_codes = [keep.tile([P, 2 * P], U32, name="wv_codes%d" % h, align_bytes=64) for h in range(2)]
         wv_plane = [keep.tile([P, 2 * P], U8, name="wv_plane%d" % h, align_bytes=64) for h in range(2)]
 
         def round_wv(copy, a, h):
@@ -141,7 +135,7 @@ def tile_list_hwayreluP_kernel(tc, xT, wgt, wk_words, wk_scales, wv, bg, res, of
         def quantise_wv(h):
             nc.vector.quantize_mx(out=wv_codes[h][:].bitcast(FP8X4), scales=wv_plane[h][:], in_=wv_bf[h][:])
 
-        gate = {c: keep.tile([P, SLOTS, C], F32, name="gate%d" % c, tag="shared%d" % c) for c in range(1, CHUNKS)}
+        gate = {c: keep.tile([P, SLOTS, C], F32, name="gate%d" % c, tag="shared%d" % c) for c in range(CHUNKS)}
         step = {}
         y = [keep.tile([P, SLOTS, C], F32, name="y%d" % c) for c in range(CHUNKS)]
         value_banks = {}
@@ -181,10 +175,7 @@ def tile_list_hwayreluP_kernel(tc, xT, wgt, wk_words, wk_scales, wv, bg, res, of
                 )
 
         def subtract_carried(c):
-            if c == 1:
-                step[c] = after_wv.tile([P, SLOTS, C], F32, name="step1", align_bytes=64, offset=0)
-            else:
-                step[c] = keep.tile([P, SLOTS, C], F32, name="step%d" % c, tag="shared%d" % (c - 1))
+            step[c] = keep.tile([P, SLOTS, C], F32, name="step%d" % c, tag="shared%d" % (c - 1))
             for h in range(2):
                 nc.vector.scalar_tensor_tensor(
                     step[c][:, PAIRS[h], :], value_banks[c][h][:], 0.0, carried[c][:, PAIRS[h], :], ALU.max, ALU.subtract
@@ -222,13 +213,13 @@ def tile_list_hwayreluP_kernel(tc, xT, wgt, wk_words, wk_scales, wv, bg, res, of
 
         gather(0, 0, J // 2)
         gather(0, J // 2, J)
-        gather(1, 0, J // 2)
-        gather(1, J // 2, J)
-        round_x_pair(0, LOWER)
-        round_x_pair(1, LOWER)
-        gather(2, 0, C)
-        gather(2, C, 2 * C)
-        gather(2, 2 * C, J)
+        gather(1, 0, C)
+        gather(1, C, 2 * C)
+        gather(1, 2 * C, J)
+        for c in range(CHUNKS):
+            round_x_pair(c, LOWER)
+        gather(2, 0, 3 * C)
+        gather(2, 3 * C, J)
         wk_plane = keep.tile([P, N], U8, name="wk_plane", tag="tokens2", align_bytes=64)
         nc.vector.tensor_copy(
             wk_plane[:].rearrange("p (t m) -> p t m", t=SLOTS),
@@ -240,15 +231,12 @@ def tile_list_hwayreluP_kernel(tc, xT, wgt, wk_words, wk_scales, wv, bg, res, of
         gather(3, C, 2 * C)
         gather(3, 2 * C, 3 * C)
         round_x_pair(0, UPPER)
-        round_x_pair(1, UPPER)
         quantise_x(0)
-        gather(3, 3 * C, J)
-        round_wv(nc.scalar.copy, 1, 0)
+        round_wv(nc.vector.tensor_copy, 1, 0)
         round_wv(nc.vector.tensor_copy, 1, 1)
-        gate[0] = after_wv.tile([P, SLOTS, C], F32, name="gate0", align_bytes=64, offset=0)
-        carry_gate = after_wv.tile([P, 2, C], F32, name="carry_gate", align_bytes=64, offset=4096)
-        wv_codes[1] = after_wv.tile([P, 2 * P], U32, name="wv_codes1", align_bytes=64, offset=7168)
-        x_codes[1] = after_wv.tile([P, C], U32, name="x_codes1", align_bytes=64, offset=6144)
+        round_x_pair(1, UPPER)
+        round_x_pair(2, UPPER)
+        carry_gate = keep.tile([P, 2, C], F32, name="carry_gate")
         minus_bias = keep.tile([P, SLOTS], F32, name="minus_bias")
         nc.scalar.mul(minus_bias[:], bias[:], -1.0)
         gate_products(0, (2, 3, 0, 1))
@@ -260,13 +248,13 @@ def tile_list_hwayreluP_kernel(tc, xT, wgt, wk_words, wk_scales, wv, bg, res, of
         quantise_wv(0)
         quantise_wv(1)
         quantise_x(1)
+        quantise_x(2)
+        gather(3, 3 * C, J)
         value_products(0)
-        x_bf[2] = keep.tile([P, C * SLOTS], BF16, name="x_bf2", tag="wv_bf0", align_bytes=64)
-        round_x(2)
-        x_bf[3] = keep.tile([P, C * SLOTS], BF16, name="x_bf3", tag="x_bf1", align_bytes=64)
+        round_x_pair(3, UPPER)
 
         whole = slice(0, C)
-        kept = keep.tile([P, 2, C], F32, name="kept", tag="wv_bf1", align_bytes=64)
+        kept = keep.tile([P, 2, C], F32, name="kept", tag="x_bf2", align_bytes=64)
         nc.gpsimd.tensor_tensor(kept[:], carry_gate[:], carried[0][:, UPPER, :], ALU.mult)
         step[0] = keep.tile([P, SLOTS, C], F32, name="step0")
         nc.vector.scalar_tensor_tensor(
@@ -278,7 +266,6 @@ def tile_list_hwayreluP_kernel(tc, xT, wgt, wk_words, wk_scales, wv, bg, res, of
         value_products(1)
         gate_products(1, range(SLOTS))
         open_gates(1, range(SLOTS))
-        round_x(3)
         apply_gate(0, LOWER, whole)
         nc.vector.tensor_tensor(y[0][:, UPPER, :], step[0][:, UPPER, :], kept[:], ALU.add)
         add_carried(nc.gpsimd, 0, LOWER, whole)
@@ -286,7 +273,8 @@ def tile_list_hwayreluP_kernel(tc, xT, wgt, wk_words, wk_scales, wv, bg, res, of
         store_y(0, whole)
         round_y(nc.scalar.copy, 0, whole)
         for c in range(1, LAST):
-            quantise_x(c + 1)
+            if c == 1:
+                quantise_x(LAST)
             value_products(c + 1)
             gate_products(c + 1, range(SLOTS))
             open_gates(c + 1, range(SLOTS))

@@ -83,8 +83,8 @@ def tile_list_hwayreluP_kernel(tc, xT, wgt, wk_words, wk_scales, wv, bg, res, of
 
         wk_codes = keep.tile([P, 2 * N], U8, name="wk_codes", align_bytes=64)
         nc.vector.tensor_copy(
-            wk_codes[:].rearrange("p (t m b) -> p t m b", t=SLOTS, b=2),
-            wk_raw[:].rearrange("p (m t b) -> p t m b", t=SLOTS, b=2),
+            wk_codes[:].bitcast(U16).rearrange("p (t m) -> p t m", t=SLOTS),
+            wk_raw[:].bitcast(U16).rearrange("p (m t) -> p t m", t=SLOTS),
         )
 
         early = keep.tile([P, 2, J], F32, name="early")
@@ -193,8 +193,8 @@ def tile_list_hwayreluP_kernel(tc, xT, wgt, wk_words, wk_scales, wv, bg, res, of
         y_codes = keep.tile([P, J], U32, name="y_codes", align_bytes=64)
         y_plane = keep.tile([P, J], U8, name="y_plane", align_bytes=64)
 
-        def store_y(c, cols):
-            nc.sync.dma_start(out_rows[:, :, c * C + cols.start : c * C + cols.stop], y[c][:, :, cols])
+        def store_y(c, slots):
+            nc.sync.dma_start(out_rows[:, slots, c * C : (c + 1) * C], y[c][:, slots, :])
 
         def round_y(copy, c, cols):
             interleave(copy, y_bf[:, SLOTS * (c * C + cols.start) : SLOTS * (c * C + cols.stop)], y[c][:, :, cols])
@@ -254,6 +254,7 @@ def tile_list_hwayreluP_kernel(tc, xT, wgt, wk_words, wk_scales, wv, bg, res, of
         round_x_pair(3, UPPER)
 
         whole = slice(0, C)
+        every = slice(0, SLOTS)
         kept = keep.tile([P, 2, C], F32, name="kept", tag="x_bf2", align_bytes=64)
         nc.gpsimd.tensor_tensor(kept[:], carry_gate[:], carried[0][:, UPPER, :], ALU.mult)
         step[0] = keep.tile([P, SLOTS, C], F32, name="step0")
@@ -270,7 +271,7 @@ def tile_list_hwayreluP_kernel(tc, xT, wgt, wk_words, wk_scales, wv, bg, res, of
         nc.vector.tensor_tensor(y[0][:, UPPER, :], step[0][:, UPPER, :], kept[:], ALU.add)
         add_carried(nc.gpsimd, 0, LOWER, whole)
         subtract_carried(1)
-        store_y(0, whole)
+        store_y(0, every)
         round_y(nc.scalar.copy, 0, whole)
         for c in range(1, LAST):
             if c == 1:
@@ -286,20 +287,20 @@ def tile_list_hwayreluP_kernel(tc, xT, wgt, wk_words, wk_scales, wv, bg, res, of
             add_carried(nc.vector, c, LOWER, whole)
             add_carried(nc.gpsimd, c, UPPER, whole)
             subtract_carried(c + 1)
-            store_y(c, whole)
+            store_y(c, every)
             round_y(nc.scalar.copy, c, whole)
 
-        every = slice(0, SLOTS)
         first, second = slice(0, C // 2), slice(C // 2, C)
         quantise_y(1, whole)
         store_words(1)
-        apply_gate(LAST, every, first)
-        apply_gate(LAST, every, second)
-        add_carried(nc.vector, LAST, every, first)
-        store_y(LAST, first)
+        apply_gate(LAST, LOWER, whole)
+        apply_gate(LAST, UPPER, whole)
+        add_carried(nc.vector, LAST, LOWER, whole)
+        store_y(LAST, LOWER)
+        add_carried(nc.vector, LAST, UPPER, first)
         round_y(nc.scalar.copy, LAST, first)
-        add_carried(nc.vector, LAST, every, second)
-        store_y(LAST, second)
+        add_carried(nc.vector, LAST, UPPER, second)
+        store_y(LAST, UPPER)
         quantise_y(2, whole)
         store_words(2)
         round_y(nc.vector.tensor_copy, LAST, second)

@@ -58,8 +58,8 @@ def tile_list_hwayreluP_kernel(tc, xT, wgt, wk_words, wk_scales, wv, bg, res, of
             nc.sync.dma_start(tokens[i][:], x_rows[:, i, :])
         nc.sync.dma_start(wv_raw[:, 0], wv_rows[:, 0])
         nc.sync.dma_start(tokens[SLOTS - 1][:], x_rows[:, SLOTS - 1, :])
-        nc.sync.dma_start(bias[:], bg.rearrange("(p t) -> p t", t=SLOTS))
         nc.sync.dma_start(wv_raw[:, 1], wv_rows[:, 1])
+        nc.sync.dma_start(bias[:], bg.rearrange("(p t) -> p t", t=SLOTS))
         res_rows = res.rearrange("(p t) j -> p t j", t=SLOTS)
         carried = [keep.tile([P, SLOTS, C], F32, name="carried%d" % c) for c in range(CHUNKS)]
         for c in range(CHUNKS):

@@ -42,7 +42,7 @@ def tile_list_hwayreluP_kernel(tc, xT, wgt, wk_words, wk_scales, wv, bg, res, of
         wk_raw = keep.tile([P, 2 * N], U8, name="wk_raw", align_bytes=64)
         nc.sync.dma_start(wk_raw[:].bitcast(I32), wk_words[0].bitcast(I32))
         wk_plane_raw = keep.tile([P, N], U8, name="wk_plane_raw", align_bytes=64)
-        nc.vector.memset(wk_plane_raw[:].bitcast(U32), 0)
+        nc.gpsimd.memset(wk_plane_raw[:].bitcast(U32), 0)
         for q in range(QUADRANTS):
             nc.scalar.dma_start(
                 wk_plane_raw[32 * q : 32 * q + 4, :].bitcast(I32), wk_scales[0, 4 * q : 4 * q + 4, :].bitcast(I32)
@@ -85,6 +85,12 @@ def tile_list_hwayreluP_kernel(tc, xT, wgt, wk_words, wk_scales, wv, bg, res, of
         nc.vector.tensor_copy(
             wk_codes[:].bitcast(U16).rearrange("p (t m) -> p t m", t=SLOTS),
             wk_raw[:].bitcast(U16).rearrange("p (m t) -> p t m", t=SLOTS),
+        )
+
+        wk_plane = keep.tile([P, N], U8, name="wk_plane", align_bytes=64)
+        nc.vector.tensor_copy(
+            wk_plane[:].rearrange("p (t m) -> p t m", t=SLOTS),
+            wk_plane_raw[:].rearrange("p (m t) -> p t m", t=SLOTS),
         )
 
         early = keep.tile([P, 2, J], F32, name="early")
@@ -220,11 +226,6 @@ def tile_list_hwayreluP_kernel(tc, xT, wgt, wk_words, wk_scales, wv, bg, res, of
             round_x_pair(c, LOWER)
         gather(2, 0, 3 * C)
         gather(2, 3 * C, J)
-        wk_plane = keep.tile([P, N], U8, name="wk_plane", tag="tokens2", align_bytes=64)
-        nc.vector.tensor_copy(
-            wk_plane[:].rearrange("p (t m) -> p t m", t=SLOTS),
-            wk_plane_raw[:].rearrange("p (m t) -> p t m", t=SLOTS),
-        )
         round_wv(nc.scalar.copy, 0, 0)
         round_wv(nc.scalar.copy, 0, 1)
         gather(3, 0, C)

@@ -36,9 +36,9 @@ def tile_list_hwayreluP_kernel(tc, xT, wgt, wk_words, wk_scales, wv, bg, res, of
         gate_psum = ctx.enter_context(tc.psum_pool(name="gate_psum", bufs=1))
 
         offsets = keep.tile([P, J // LIST_ROWS], U16, name="offsets")
-        nc.sync.dma_start(offsets[:], offs)
         weight_rows = keep.tile([P, J // LIST_ROWS], F32, name="weight_rows", align_bytes=64)
-        nc.sync.dma_start(weight_rows[:], wgt.rearrange("(g r) j -> g r j", r=LIST_ROWS)[:, 0, :])
+        nc.sync.dma_start(weight_rows[:], wgt.rearrange("r (a j) -> (r a) j", a=2)[0 : 2 * P : LIST_ROWS + 1, :])
+        nc.sync.dma_start(offsets[:], offs)
         wk_raw = keep.tile([P, 2 * N], U8, name="wk_raw", align_bytes=64)
         nc.sync.dma_start(wk_raw[:].bitcast(I32), wk_words[0].bitcast(I32))
         wk_plane_raw = keep.tile([P, N], U8, name="wk_plane_raw", align_bytes=64)

@@ -26,6 +26,7 @@ CHUNKS = J // C
 LAST = CHUNKS - 1
 LOWER, UPPER = slice(0, 2), slice(2, 4)
 PAIRS = (LOWER, UPPER)
+END_CUT = 160
 
 
 def tile_list_hwayreluP_kernel(tc, xT, wgt, wk_words, wk_scales, wv, bg, res, offs, out_0, out_1, out_2):
@@ -211,10 +212,10 @@ def tile_list_hwayreluP_kernel(tc, xT, wgt, wk_words, wk_scales, wv, bg, res, of
                 out=y_codes[:, j0:j1].bitcast(FP8X4), scales=y_plane[:, j0:j1], in_=y_bf[:, SLOTS * j0 : SLOTS * j1]
             )
 
-        def store_words(c):
+        def store_words(first, last):
             nc.sync.dma_start(
-                out_words[:, SLOTS * c * C : SLOTS * (c + 1) * C].bitcast(I32),
-                y_codes[:, c * C : (c + 1) * C].bitcast(I32),
+                out_words[:, SLOTS * first * C : SLOTS * (last + 1) * C].bitcast(I32),
+                y_codes[:, first * C : (last + 1) * C].bitcast(I32),
             )
 
         gather(0, 0, J // 2)
@@ -283,7 +284,7 @@ def tile_list_hwayreluP_kernel(tc, xT, wgt, wk_words, wk_scales, wv, bg, res, of
             apply_gate(c, LOWER, whole)
             if c == LAST - 1:
                 quantise_y(0, whole)
-                store_words(0)
+                store_words(0, 0)
             apply_gate(c, UPPER, whole)
             add_carried(nc.vector, c, LOWER, whole)
             add_carried(nc.gpsimd, c, UPPER, whole)
@@ -291,23 +292,21 @@ def tile_list_hwayreluP_kernel(tc, xT, wgt, wk_words, wk_scales, wv, bg, res, of
             store_y(c, every)
             round_y(nc.scalar.copy, c, whole)
 
-        first, second = slice(0, C // 2), slice(C // 2, C)
-        quantise_y(1, whole)
-        store_words(1)
+        on_scalar, on_vector = slice(0, END_CUT), slice(END_CUT, C)
         apply_gate(LAST, LOWER, whole)
         apply_gate(LAST, UPPER, whole)
         add_carried(nc.vector, LAST, LOWER, whole)
         store_y(LAST, LOWER)
-        add_carried(nc.vector, LAST, UPPER, first)
-        round_y(nc.scalar.copy, LAST, first)
-        add_carried(nc.vector, LAST, UPPER, second)
+        add_carried(nc.vector, LAST, UPPER, on_scalar)
+        round_y(nc.scalar.copy, LAST, on_scalar)
+        add_carried(nc.vector, LAST, UPPER, on_vector)
         store_y(LAST, UPPER)
+        quantise_y(1, whole)
+        round_y(nc.vector.tensor_copy, LAST, on_vector)
         quantise_y(2, whole)
-        store_words(2)
-        round_y(nc.vector.tensor_copy, LAST, second)
-        quantise_y(LAST, first)
-        quantise_y(LAST, second)
-        store_words(LAST)
+        store_words(1, 2)
+        quantise_y(LAST, whole)
+        store_words(LAST, LAST)
         for q in range(QUADRANTS):
             queue = nc.scalar if q % 2 else nc.sync
             queue.dma_start(out_2[0, 4 * q : 4 * q + 4, :].bitcast(I32), y_plane[32 * q : 32 * q + 4, :].bitcast(I32))

@@ -198,7 +198,7 @@ def tile_list_hwayreluP_kernel(tc, xT, wgt, wk_words, wk_scales, wv, bg, res, of
         out_words = out_1[0].rearrange("p j i -> p (j i)")
         y_bf = keep.tile([P, J * SLOTS], BF16, name="y_bf", align_bytes=64)
         y_codes = keep.tile([P, J], U32, name="y_codes", align_bytes=64)
-        y_plane = keep.tile([P, J], U8, name="y_plane", align_bytes=64)
+        y_plane = keep.tile([P, 2 * C], U8, name="y_plane", align_bytes=64)
 
         def store_y(c, slots):
             nc.sync.dma_start(out_rows[:, slots, c * C : (c + 1) * C], y[c][:, slots, :])
@@ -209,7 +209,7 @@ def tile_list_hwayreluP_kernel(tc, xT, wgt, wk_words, wk_scales, wv, bg, res, of
         def quantise_y(c, cols):
             j0, j1 = c * C + cols.start, c * C + cols.stop
             nc.vector.quantize_mx(
-                out=y_codes[:, j0:j1].bitcast(FP8X4), scales=y_plane[:, j0:j1], in_=y_bf[:, SLOTS * j0 : SLOTS * j1]
+                out=y_codes[:, j0:j1].bitcast(FP8X4), scales=y_plane[4 * (c // 2) :, j0 % (2 * C) : j0 % (2 * C) + j1 - j0], in_=y_bf[:, SLOTS * j0 : SLOTS * j1]
             )
 
         def store_words(first, last):
@@ -309,4 +309,7 @@ def tile_list_hwayreluP_kernel(tc, xT, wgt, wk_words, wk_scales, wv, bg, res, of
         store_words(LAST, LAST)
         for q in range(QUADRANTS):
             queue = nc.scalar if q % 2 else nc.sync
-            queue.dma_start(out_2[0, 4 * q : 4 * q + 4, :].bitcast(I32), y_plane[32 * q : 32 * q + 4, :].bitcast(I32))
+            queue.dma_start(
+                out_2[0, 4 * q : 4 * q + 4, :].bitcast(I32).rearrange("r (a w) -> a r w", a=2),
+                y_plane[32 * q : 32 * q + 8, :].bitcast(I32),
+            )

from contextlib import ExitStack

import concourse.mybir as mybir

K, N, T, J = 512, 512, 2048, 1024
FLOPS = 2 * 2 * K * N * J

F32 = mybir.dt.float32
BF16 = mybir.dt.bfloat16
I32 = mybir.dt.int32
U32 = mybir.dt.uint32
U16 = mybir.dt.uint16
U8 = mybir.dt.uint8
FP8X4 = mybir.dt.float8_e4m3fn_x4
FP4X4 = mybir.dt.float4_e2m1fn_x4
ALU = mybir.AluOpType
ACT = mybir.ActivationFunctionType

P = 128
SLOTS = 4
LIST_ROWS = 16
QUADRANTS = 4
RUN = 4
C = 256
CHUNKS = J // C
LAST = CHUNKS - 1
LOWER, UPPER = slice(0, 2), slice(2, 4)
PAIRS = (LOWER, UPPER)
END_CUT = 160


def tile_list_hwayreluP_kernel(tc, xT, wgt, wk_words, wk_scales, wv, bg, res, offs, out_0, out_1, out_2):
    nc = tc.nc
    with ExitStack() as ctx:
        keep = ctx.enter_context(tc.tile_pool(name="keep", bufs=1))
        psum = ctx.enter_context(tc.psum_pool(name="psum", bufs=2))
        gate_psum = ctx.enter_context(tc.psum_pool(name="gate_psum", bufs=1))

        offsets = keep.tile([P, J // LIST_ROWS], U16, name="offsets")
        weight_rows = keep.tile([P, J // LIST_ROWS], F32, name="weight_rows", align_bytes=64)
        nc.sync.dma_start(weight_rows[:], wgt.rearrange("r (a j) -> (r a) j", a=2)[0 : 2 * P : LIST_ROWS + 1, :])
        nc.sync.dma_start(offsets[:], offs)
        wk_raw = keep.tile([P, 2 * N], U8, name="wk_raw", align_bytes=64)
        nc.sync.dma_start(wk_raw[:].bitcast(I32), wk_words[0].bitcast(I32))
        wk_plane_raw = keep.tile([P, N], U8, name="wk_plane_raw", align_bytes=64)
        nc.gpsimd.memset(wk_plane_raw[:].bitcast(U32), 0)
        for q in range(QUADRANTS):
            nc.scalar.dma_start(
                wk_plane_raw[32 * q : 32 * q + 4, :].bitcast(I32), wk_scales[0, 4 * q : 4 * q + 4, :].bitcast(I32)
            )

        pick_weights = keep.tile([P, J], F32, name="pick_weights", align_bytes=64)
        x_rows = xT.rearrange("(p i) t -> p i t", i=SLOTS)
        tokens = [keep.tile([P, T], F32, name="tokens%d" % i, align_bytes=64) for i in range(SLOTS)]
        bias = keep.tile([P, SLOTS], F32, name="bias")
        wv_raw = keep.tile([P, 2, SLOTS, N // 2], F32, name="wv_raw")
        wv_rows = wv.rearrange("(p i) (a n) -> p a i n", i=SLOTS, a=2)
        for i in range(SLOTS - 1):
            nc.sync.dma_start(tokens[i][:], x_rows[:, i, :])
        nc.sync.dma_start(wv_raw[:, 0], wv_rows[:, 0])
        nc.sync.dma_start(tokens[SLOTS - 1][:], x_rows[:, SLOTS - 1, :])
        nc.sync.dma_start(wv_raw[:, 1], wv_rows[:, 1])
        nc.sync.dma_start(bias[:], bg.rearrange("(p t) -> p t", t=SLOTS))
        res_rows = res.rearrange("(p t) j -> p t j", t=SLOTS)
        carried = [keep.tile([P, SLOTS, C], F32, name="carried%d" % c) for c in range(CHUNKS)]
        for c in range(CHUNKS):
            nc.sync.dma_start(carried[c][:], res_rows[:, :, c * C : (c + 1) * C])

        warm = keep.tile([P, 2], F32, name="warm")
        nc.vector.memset(warm[:, 0:1], 0.0)
        nc.scalar.activation(warm[:, 1:2], warm[:, 0:1], ACT.Sigmoid)

        turned = keep.tile([P, 64], F32, name="turned", align_bytes=64)
        for s in range(2):
            nc.vector.transpose(turned[:, 32 * s : 32 * (s + 1)], weight_rows[:, 32 * s : 32 * (s + 1)])
        repeated = keep.tile([P, J], F32, name="repeated", align_bytes=64)
        for u, copy in enumerate((nc.vector.tensor_copy, nc.scalar.copy)):
            half = slice(u * J // 2, (u + 1) * J // 2)
            copy(
                repeated[:, half].rearrange("p (b q r) -> p b q r", q=4, r=LIST_ROWS),
                turned[:].rearrange("p (q b) -> p b q", q=4)[:, 8 * u : 8 * (u + 1), :].unsqueeze(3).to_broadcast([P, 8, 4, LIST_ROWS]),
            )
            nc.vector.transpose(pick_weights[:, half], repeated[:, half])

        wk_codes = keep.tile([P, 2 * N], U8, name="wk_codes", align_bytes=64)
        nc.vector.tensor_copy(
            wk_codes[:].bitcast(U16).rearrange("p (t m) -> p t m", t=SLOTS),
            wk_raw[:].bitcast(U16).rearrange("p (m t) -> p t m", t=SLOTS),
        )

        wk_plane = keep.tile([P, N], U8, name="wk_plane", align_bytes=64)
        nc.vector.tensor_copy(
            wk_plane[:].rearrange("p (t m) -> p t m", t=SLOTS),
            wk_plane_raw[:].rearrange("p (m t) -> p t m", t=SLOTS),
        )

        early = keep.tile([P, 2, J], F32, name="early")
        late = keep.tile([P, 7, C], F32, name="late")
        late_blocks = {0: (1, 4), 1: (2, 5), 2: (3, 6), 3: (0, 3)}
        x_bf = [keep.tile([P, C * SLOTS], BF16, name="x_bf%d" % c, align_bytes=64) for c in range(CHUNKS)]
        x_codes = {c: keep.tile([P, C], U32, name="x_codes%d" % c, align_bytes=64) for c in range(CHUNKS)}
        x_plane = [keep.tile([P, C], U8, name="x_plane%d" % c, align_bytes=64) for c in range(CHUNKS)]

        def gather(i, j0, j1):
            window = tokens[i][:].indirect(offsets[:, j0 // LIST_ROWS : j1 // LIST_ROWS])
            if i < 2:
                out = early[:, i, j0:j1]
            else:
                block = late_blocks[j0 // C][i - 2]
                out = late[:, block : block + (j1 - j0) // C, :].rearrange("p b c -> p (b c)")
            nc.vector.tensor_tensor(out, window, pick_weights[:, j0:j1], ALU.mult)

        def interleave(copy, dst, src):
            copy(
                dst.rearrange("p (c e t) -> p c t e", e=RUN, t=SLOTS),
                src.rearrange("p t (c e) -> p c t e", e=RUN),
            )

        def round_x_pair(c, slots):
            if slots == LOWER:
                pair = early[:, :, c * C : (c + 1) * C]
            else:
                pair = late[:, late_blocks[c][0] : late_blocks[c][1] + 1 : 3, :]
            nc.scalar.copy(
                x_bf[c][:].rearrange("p (c t) -> p c t", t=SLOTS)[:, :, slots],
                pair.rearrange("p t c -> p c t"),
            )

        def quantise_x(c):
            nc.vector.quantize_mx(out=x_codes[c][:].bitcast(FP8X4), scales=x_plane[c][:], in_=x_bf[c][:])

        wv_bf = [keep.tile([P, 2 * P * SLOTS], BF16, name="wv_bf%d" % h, align_bytes=64) for h in range(2)]
        wv_codes = [keep.tile([P, 2 * P], U32, name="wv_codes%d" % h, align_bytes=64) for h in range(2)]
        wv_plane = [keep.tile([P, 2 * P], U8, name="wv_plane%d" % h, align_bytes=64) for h in range(2)]

        def round_wv(copy, a, h):
            copy(
                wv_bf[h][:].rearrange("p (u m i) -> p m i u", u=2, i=SLOTS)[:, a * P // 2 : (a + 1) * P // 2],
                wv_raw[:, a].rearrange("p i (m t) -> p m i t", t=SLOTS)[:, :, :, PAIRS[h]],
            )

        def quantise_wv(h):
            nc.vector.quantize_mx(out=wv_codes[h][:].bitcast(FP8X4), scales=wv_plane[h][:], in_=wv_bf[h][:])

        gate = {c: keep.tile([P, SLOTS, C], F32, name="gate%d" % c, tag="shared%d" % c) for c in range(CHUNKS)}
        step = {}
        y = [keep.tile([P, SLOTS, C], F32, name="y%d" % c) for c in range(CHUNKS)]
        value_banks = {}
        gate_banks = {}

        def gate_products(c, order):
            gate_banks[c] = [gate_psum.tile([P, 2, C], F32, name="ke%d" % h) for h in range(2)]
            for t in order:
                nc.tensor.matmul_mx(
                    out=gate_banks[c][t // 2][:, t % 2, :],
                    lhsT=wk_codes[:, 2 * P * t : 2 * P * (t + 1)].bitcast(FP4X4),
                    lhsT_scale=wk_plane[:, P * t : P * (t + 1)],
                    rhs=x_codes[c][:].bitcast(FP8X4),
                    rhs_scale=x_plane[c][:],
                    start=True,
                    stop=True,
                )

        def open_gates(c, order):
            for t in order:
                nc.scalar.activation(
                    gate[c][:, t, :], gate_banks[c][t // 2][:, t % 2, :], ACT.Sigmoid, bias=bias[:, t : t + 1]
                )

        def value_products(c):
            value_banks[c] = [psum.tile([P, 2, C], F32, name="ve%d" % h) for h in range(2)]
            for t in range(SLOTS):
                columns = slice(P * (t % 2), P * (t % 2 + 1))
                nc.tensor.matmul_mx(
                    out=value_banks[c][t // 2][:, t % 2, :],
                    lhsT=wv_codes[t // 2][:, columns].bitcast(FP8X4),
                    lhsT_scale=wv_plane[t // 2][:, columns],
                    rhs=x_codes[c][:].bitcast(FP8X4),
                    rhs_scale=x_plane[c][:],
                    start=True,
                    stop=True,
                )

        def subtract_carried(c):
            step[c] = keep.tile([P, SLOTS, C], F32, name="step%d" % c, tag="shared%d" % (c - 1))
            for h in range(2):
                nc.vector.scalar_tensor_tensor(
                    step[c][:, PAIRS[h], :], value_banks[c][h][:], 0.0, carried[c][:, PAIRS[h], :], ALU.max, ALU.subtract
                )

        def apply_gate(c, slots, cols):
            nc.vector.tensor_tensor(step[c][:, slots, cols], step[c][:, slots, cols], gate[c][:, slots, cols], ALU.mult)

        def add_carried(engine, c, slots, cols):
            engine.tensor_tensor(y[c][:, slots, cols], step[c][:, slots, cols], carried[c][:, slots, cols], ALU.add)

        out_rows = out_0.rearrange("(p t) j -> p t j", t=SLOTS)
        out_words = out_1[0].rearrange("p j i -> p (j i)")
        y_bf = keep.tile([P, J * SLOTS], BF16, name="y_bf", align_bytes=64)
        y_codes = keep.tile([P, J], U32, name="y_codes", align_bytes=64)
        y_plane = keep.tile([P, 2 * C], U8, name="y_plane", align_bytes=64)

        def store_y(c, slots):
            nc.sync.dma_start(out_rows[:, slots, c * C : (c + 1) * C], y[c][:, slots, :])

        def round_y(copy, c, cols):
            interleave(copy, y_bf[:, SLOTS * (c * C + cols.start) : SLOTS * (c * C + cols.stop)], y[c][:, :, cols])

        def quantise_y(c, cols):
            j0, j1 = c * C + cols.start, c * C + cols.stop
            nc.vector.quantize_mx(
                out=y_codes[:, j0:j1].bitcast(FP8X4), scales=y_plane[4 * (c // 2) :, j0 % (2 * C) : j0 % (2 * C) + j1 - j0], in_=y_bf[:, SLOTS * j0 : SLOTS * j1]
            )

        def store_words(first, last):
            nc.sync.dma_start(
                out_words[:, SLOTS * first * C : SLOTS * (last + 1) * C].bitcast(I32),
                y_codes[:, first * C : (last + 1) * C].bitcast(I32),
            )

        gather(0, 0, J // 2)
        gather(0, J // 2, J)
        gather(1, 0, C)
        gather(1, C, 2 * C)
        gather(1, 2 * C, J)
        for c in range(CHUNKS):
            round_x_pair(c, LOWER)
        gather(2, 0, 3 * C)
        gather(2, 3 * C, J)
        round_wv(nc.scalar.copy, 0, 0)
        round_wv(nc.scalar.copy, 0, 1)
        gather(3, 0, C)
        gather(3, C, 2 * C)
        gather(3, 2 * C, 3 * C)
        round_x_pair(0, UPPER)
        quantise_x(0)
        round_wv(nc.vector.tensor_copy, 1, 0)
        round_wv(nc.vector.tensor_copy, 1, 1)
        round_x_pair(1, UPPER)
        round_x_pair(2, UPPER)
        carry_gate = keep.tile([P, 2, C], F32, name="carry_gate")
        minus_bias = keep.tile([P, SLOTS], F32, name="minus_bias")
        nc.scalar.mul(minus_bias[:], bias[:], -1.0)
        gate_products(0, (2, 3, 0, 1))
        for t in (2, 3):
            nc.scalar.activation(
                carry_gate[:, t - 2, :], gate_banks[0][1][:, t - 2, :], ACT.Sigmoid, bias=minus_bias[:, t : t + 1], scale=-1.0
            )
        open_gates(0, (2, 3, 0, 1))
        quantise_wv(0)
        quantise_wv(1)
        quantise_x(1)
        quantise_x(2)
        gather(3, 3 * C, J)
        value_products(0)
        round_x_pair(3, UPPER)

        whole = slice(0, C)
        every = slice(0, SLOTS)
        kept = keep.tile([P, 2, C], F32, name="kept", tag="x_bf2", align_bytes=64)
        nc.gpsimd.tensor_tensor(kept[:], carry_gate[:], carried[0][:, UPPER, :], ALU.mult)
        step[0] = keep.tile([P, SLOTS, C], F32, name="step0")
        nc.vector.scalar_tensor_tensor(
            step[0][:, LOWER, :], value_banks[0][0][:], 0.0, carried[0][:, LOWER, :], ALU.max, ALU.subtract
        )
        nc.vector.scalar_tensor_tensor(
            step[0][:, UPPER, :], value_banks[0][1][:], 0.0, gate[0][:, UPPER, :], ALU.max, ALU.mult
        )
        value_products(1)
        gate_products(1, range(SLOTS))
        open_gates(1, range(SLOTS))
        apply_gate(0, LOWER, whole)
        nc.vector.tensor_tensor(y[0][:, UPPER, :], step[0][:, UPPER, :], kept[:], ALU.add)
        add_carried(nc.gpsimd, 0, LOWER, whole)
        subtract_carried(1)
        store_y(0, every)
        round_y(nc.scalar.copy, 0, whole)
        for c in range(1, LAST):
            if c == 1:
                quantise_x(LAST)
            value_products(c + 1)
            gate_products(c + 1, range(SLOTS))
            open_gates(c + 1, range(SLOTS))
            apply_gate(c, LOWER, whole)
            if c == LAST - 1:
                quantise_y(0, whole)
                store_words(0, 0)
            apply_gate(c, UPPER, whole)
            add_carried(nc.vector, c, LOWER, whole)
            add_carried(nc.gpsimd, c, UPPER, whole)
            subtract_carried(c + 1)
            store_y(c, every)
            round_y(nc.scalar.copy, c, whole)

        on_scalar, on_vector = slice(0, END_CUT), slice(END_CUT, C)
        apply_gate(LAST, LOWER, whole)
        apply_gate(LAST, UPPER, whole)
        add_carried(nc.vector, LAST, LOWER, whole)
        store_y(LAST, LOWER)
        add_carried(nc.vector, LAST, UPPER, on_scalar)
        round_y(nc.scalar.copy, LAST, on_scalar)
        add_carried(nc.vector, LAST, UPPER, on_vector)
        store_y(LAST, UPPER)
        quantise_y(1, whole)
        round_y(nc.vector.tensor_copy, LAST, on_vector)
        quantise_y(2, whole)
        store_words(1, 2)
        quantise_y(LAST, whole)
        store_words(LAST, LAST)
        for q in range(QUADRANTS):
            queue = nc.scalar if q % 2 else nc.sync
            queue.dma_start(
                out_2[0, 4 * q : 4 * q + 4, :].bitcast(I32).rearrange("r (a w) -> a r w", a=2),
                y_plane[32 * q : 32 * q + 8, :].bitcast(I32),
            )
